import numpy as np
import ml_dtypes


def mxq(x, axis, fmt="e4m3"):
    dtype, down = {"e4m3": (ml_dtypes.float8_e4m3fn, 7), "e5m2": (ml_dtypes.float8_e5m2, 14)}[fmt]
    v = np.moveaxis(np.asarray(x, np.float32).astype(ml_dtypes.bfloat16).astype(np.float64), axis, -1)
    blocks = v.reshape(v.shape[:-1] + (-1, 32))
    amax = np.abs(blocks).max(-1, keepdims=True)
    byte = np.maximum(np.where(amax > 0, np.frexp(amax)[1] - 1 + 127, 0) - down, 1)
    scale = np.exp2(byte - 127.0)
    codes = (blocks / scale).astype(np.float32).astype(dtype).astype(np.float64)
    return np.moveaxis((codes * scale).reshape(v.shape), -1, axis)


WIDE = False


def mx_kscale(k):
    if not WIDE:
        return np.ones(k)
    levels = np.array([30, -30])
    if k % 512:
        return np.exp2(np.random.permutation(np.resize(levels, k // 32))).repeat(32)
    a = np.empty((k // 512, 16))
    for p in range(k // 512):
        a[p, :8] = np.random.permutation(np.resize(levels, 8))
        for g in range(8):
            far = levels[np.abs(levels - a[p, g]) >= 10]
            a[p, g + 8] = far[np.random.randint(len(far))]
    return np.exp2(a.ravel()).repeat(32)


def f64(x):
    return np.asarray(x).astype(np.float64)


def striped(idx):
    return np.tile(idx.reshape(-1, 16).T, (8, 1)).astype(np.uint16)


def unstriped(offs):
    return offs[:16].T.reshape(-1).astype(np.int64)


E2M1 = np.array([0.0, 0.5, 1.0, 1.5, 2.0, 3.0, 4.0, 6.0, -0.0, -0.5, -1.0, -1.5, -2.0, -3.0, -4.0, -6.0])


def pack_weight(w, fmt):
    k, n = w.shape
    w = f64(np.asarray(w, np.float32).astype(ml_dtypes.bfloat16)).reshape(k // 32, 32, n)
    amax = np.abs(w).max(1)
    if fmt == "e4m3":
        byte = np.frexp(amax)[1] - 1 + 127 - 7
    else:
        mant, ex = np.frexp(amax / 6.0)
        byte = np.where(mant > 0.5, ex, ex - 1) + 127
    byte = np.clip(np.where(amax > 0, byte, 1), 1, 254)
    scaled = (w * np.exp2(127.0 - byte)[:, None, :]).reshape(k, n).astype(np.float32)
    by_word = np.ascontiguousarray(scaled.reshape(k // 512, 128, 4, n).transpose(0, 1, 3, 2))
    if fmt == "e4m3":
        words = by_word.astype(ml_dtypes.float8_e4m3fn).view(np.uint8)
    else:
        c = by_word.astype(ml_dtypes.float4_e2m1fn).view(np.uint8) & 0xF
        words = (c[..., 0::2] | (c[..., 1::2] << 4)).reshape(k // 512, 128, 2 * n)
    return np.ascontiguousarray(words), np.ascontiguousarray(byte.astype(np.uint8).reshape(k // 512, 16, n))


def unpack_weight(words, scales, fmt):
    g, _, n = scales.shape
    words = np.ascontiguousarray(words).reshape(g, 128, n, -1)
    if fmt == "e4m3":
        vals = words.view(ml_dtypes.float8_e4m3fn).astype(np.float64)
    else:
        nib = np.empty((g, 128, n, 4), np.uint8)
        nib[..., 0::2] = words & 0xF
        nib[..., 1::2] = words >> 4
        vals = E2M1[nib]
    vals = vals * np.repeat(np.exp2(scales.astype(np.float64) - 127.0), 8, axis=1)[..., None]
    return vals.transpose(0, 1, 3, 2).reshape(g * 512, n)


def planes(y):
    n, m = y.shape
    v = y.astype(np.float32).astype(ml_dtypes.bfloat16).astype(np.float64).reshape(n // 32, 32, m)
    top = np.abs(v).max(1)
    byte = np.clip(np.where(top > 0, np.frexp(top)[1] - 1 + 127 - 7, 1), 1, 254)
    codes = (v * np.exp2(127.0 - byte)[:, None, :]).reshape(n, m).astype(np.float32).astype(ml_dtypes.float8_e4m3fn).view(np.uint8)
    words = codes.reshape(n // 512, 128, 4, m).transpose(0, 1, 3, 2)
    return np.ascontiguousarray(words), np.ascontiguousarray(byte.astype(np.uint8).reshape(n // 512, 16, m))


K, N, T, J = 1024, 512, 2048, 1024


def setup_inputs():
    n = np.random.standard_normal
    s = mx_kscale(K)[:, None]
    m = np.exp(0.5 * n((1, J)))
    w = n((K, N)) / np.sqrt(K) / s
    w4 = pack_weight(w, "e2m1")
    wrest = w - unpack_weight(*w4, "e2m1")
    p_w8 = pack_weight(wrest, "e4m3")
    return {
        "dy": (m * n((K, J)) * s).astype(np.float32),
        "w4_words": w4[0],
        "w4_scales": w4[1],
        "w8_words": p_w8[0],
        "w8_scales": p_w8[1],
        "wgo": np.tile(np.random.uniform(0.5, 2.0, J), (128, 1)).astype(np.float32),
        "offs": striped(np.random.permutation(T)[:J]),
    }


def reference(dy, w4_words, w4_scales, w8_words, w8_scales, wgo, offs):
    idx = unstriped(offs)
    dy_ = mxq(f64(dy), 0, "e5m2")
    w4_ = unpack_weight(w4_words, w4_scales, "e2m1")
    w8_ = unpack_weight(w8_words, w8_scales, "e4m3")
    dx = w4_.T @ dy_ + w8_.T @ dy_
    out = np.zeros((N, T))
    out[:, idx] = f64(wgo)[0] * (dx)
    return (out,) + planes(out)

@@ -1,0 +1,266 @@
+from contextlib import ExitStack
+
+import concourse.mybir as mybir
+
+K, N, T, J = 1024, 512, 2048, 1024
+FLOPS = 2 * 2 * K * N * J
+
+F32 = mybir.dt.float32
+BF16 = mybir.dt.bfloat16
+I32 = mybir.dt.int32
+U32 = mybir.dt.uint32
+U16 = mybir.dt.uint16
+U8 = mybir.dt.uint8
+E4M3X4 = mybir.dt.float8_e4m3fn_x4
+E5M2X4 = mybir.dt.float8_e5m2_x4
+E2M1X4 = mybir.dt.float4_e2m1fn_x4
+MULT = mybir.AluOpType.mult
+
+P = 128
+PACK = 4
+K_PASS = P * PACK
+PASSES = K // K_PASS
+HALF = 512
+CHUNK = 512
+CHUNKS = T // CHUNK
+LINE = 4
+
+
+def tile_list_embg_res_noneP_kernel(
+    tc, dy, w4_words, w4_scales, w8_words, w8_scales, wgo, offs, out_0, out_1, out_2
+):
+    nc = tc.nc
+    with ExitStack() as ctx:
+        listp = ctx.enter_context(tc.tile_pool(name="listp", bufs=1))
+        keep = ctx.enter_context(tc.tile_pool(name="keep", bufs=1))
+        psum = ctx.enter_context(tc.psum_pool(name="psum", bufs=1))
+
+        def sb(name, shape, dtype, tag=None):
+            return keep.tile(shape, dtype, name=name, tag=tag or name, align_bytes=64)
+
+        offsets = listp.tile([P, J // 16], U16, name="offsets")
+
+        s8_raw = sb("s8_raw", [P, PASSES, N], U8)
+        s4_raw = sb("s4_raw", [P, PASSES, N], U8)
+        nc.vector.memset(s8_raw[:].rearrange("p a n -> p (a n)").bitcast(I32), 0)
+        nc.vector.memset(s4_raw[:].rearrange("p a n -> p (a n)").bitcast(I32), 0)
+
+        def load_dy(name, a, j0, width, tag=None):
+            raw = sb(name, [P, PACK, width], F32, tag)
+            rows = dy[a * K_PASS : (a + 1) * K_PASS, j0 : j0 + width]
+            nc.sync.dma_start(out=raw[:], in_=rows.rearrange("(p i) j -> p i j", i=PACK))
+            return raw
+
+        def load_scales(queue, dst, src):
+            for q in range(4):
+                queue.dma_start(
+                    out=dst[32 * q : 32 * q + 4, :, :].bitcast(I32),
+                    in_=src[:, 4 * q : 4 * q + 4, :].rearrange("a r n -> r a n").bitcast(I32),
+                )
+
+        raw00 = load_dy("raw00", 0, 0, HALF)
+        load_scales(nc.sync, s8_raw, w8_scales)
+        w8_raw = sb("w8_raw", [P, PASSES, N], I32)
+        nc.sync.dma_start(out=w8_raw[:], in_=w8_words.rearrange("a p n i -> p a (n i)").bitcast(I32))
+        w4_raw = sb("w4_raw", [P, PASSES, 2 * N], U8)
+        nc.sync.dma_start(out=w4_raw[:].bitcast(I32), in_=w4_words.rearrange("a p b -> p a b").bitcast(I32))
+        raw01a = load_dy("raw01a", 1, 0, HALF // 2)
+        load_scales(nc.sync, s4_raw, w4_scales)
+        raw01b = load_dy("raw01b", 1, HALF // 2, HALF // 2)
+        nc.sync.dma_start(offsets[:], offs)
+        wgo_sb = [sb(f"wgo{h}", [P, HALF], F32) for h in range(2)]
+        nc.sync.dma_start(out=wgo_sb[0][:], in_=wgo[:, 0:HALF])
+        raw10 = load_dy("raw10", 0, HALF, HALF)
+        raw11 = load_dy("raw11", 1, HALF, HALF, "slot_b")
+        nc.sync.dma_start(out=wgo_sb[1][:], in_=wgo[:, HALF:J])
+
+        window = {}
+        for t in (0, 1):
+            window[t] = sb(f"window{t}", [P, T], F32)
+            nc.vector.memset(window[t][:], 0.0)
+
+        w8_t = [sb(f"w8_t{u}", [P, 2, PASSES, P], I32) for u in range(2)]
+        w4_t = [sb(f"w4_t{u}", [P, 2, PASSES, 2 * P], U8) for u in range(2)]
+        s8_t = [sb(f"s8_t{u}", [P, 2, PASSES, P], U8) for u in range(2)]
+        s4_t = [sb(f"s4_t{u}", [P, 2, PASSES, P], U8) for u in range(2)]
+
+        def deal(u):
+            ts = slice(2 * u, 2 * u + 2)
+            nc.vector.tensor_copy(
+                out=w8_t[u][:], in_=w8_raw[:].rearrange("p a (m t) -> p t a m", t=PACK)[:, ts]
+            )
+            nc.vector.tensor_copy(
+                out=s8_t[u][:], in_=s8_raw[:].rearrange("p a (m t) -> p t a m", t=PACK)[:, ts]
+            )
+            nc.vector.tensor_copy(
+                out=w4_t[u][:].bitcast(U16),
+                in_=w4_raw[:].bitcast(U16).rearrange("p a (m t) -> p t a m", t=PACK)[:, ts],
+            )
+            nc.vector.tensor_copy(
+                out=s4_t[u][:], in_=s4_raw[:].rearrange("p a (m t) -> p t a m", t=PACK)[:, ts]
+            )
+
+        def interleave(copy, grouped, c0, raw, r0, width):
+            copy(
+                out=grouped[:, c0 : c0 + width, :].rearrange("p (c l) i -> p c i l", l=LINE),
+                in_=raw[:, :, r0 : r0 + width].rearrange("p i (c l) -> p c i l", l=LINE),
+            )
+
+        codes = {}
+        scales = {}
+        for h in range(2):
+            for a in range(PASSES):
+                codes[h, a] = sb(f"codes{h}{a}", [P, HALF], U32)
+                scales[h, a] = sb(f"scales{h}{a}", [P, HALF], U8)
+
+        def quantise(h, a, grouped, c0, width):
+            nc.vector.quantize_mx(
+                out=codes[h, a][:, c0 : c0 + width].bitcast(E5M2X4),
+                scales=scales[h, a][:, c0 : c0 + width],
+                in_=grouped[:].rearrange("p c i -> p (c i)"),
+            )
+
+        bank = {}
+        bank_tag = {(0, 0): "b0", (1, 0): "b1", (2, 0): "b0", (3, 0): "b1", (0, 1): "b2", (1, 1): "b0", (2, 1): "b2", (3, 1): "b1"}
+
+        def passes(t, h, a):
+            if a == 0:
+                bank[t, h] = psum.tile([P, HALF], F32, name=f"bank{t}{h}", tag=bank_tag[t, h])
+            nc.tensor.matmul_mx(
+                out=bank[t, h][:],
+                lhsT=w8_t[t // 2][:, t % 2, a, :].bitcast(E4M3X4),
+                lhsT_scale=s8_t[t // 2][:, t % 2, a, :],
+                rhs=codes[h, a][:].bitcast(E5M2X4),
+                rhs_scale=scales[h, a][:],
+                start=(a == 0),
+                stop=False,
+            )
+            nc.tensor.matmul_mx(
+                out=bank[t, h][:],
+                lhsT=w4_t[t // 2][:, t % 2, a, :].bitcast(E2M1X4),
+                lhsT_scale=s4_t[t // 2][:, t % 2, a, :],
+                rhs=codes[h, a][:].bitcast(E5M2X4),
+                rhs_scale=scales[h, a][:],
+                start=False,
+                stop=(a == PASSES - 1),
+            )
+
+        dx = {}
+
+        def empty_bank(t, h, tag=None):
+            dx[t, h] = sb(f"dx{t}{h}", [P, HALF], F32, tag)
+            nc.scalar.copy(out=dx[t, h][:], in_=bank[t, h][:])
+
+        def scatter(t, h):
+            cols = HALF // 16
+            nc.vector.tensor_tensor(
+                window[t][:].indirect(offsets[:, h * cols : (h + 1) * cols]), dx[t, h][:], wgo_sb[h][:], MULT
+            )
+
+        deal(0)
+        g00 = sb("g00", [P, HALF, PACK], BF16)
+        interleave(nc.scalar.copy, g00, 0, raw00, 0, HALF)
+        quantise(0, 0, g00, 0, HALF)
+        g01a = sb("g01a", [P, HALF // 2, PACK], BF16)
+        interleave(nc.scalar.copy, g01a, 0, raw01a, 0, HALF // 2)
+        g01b = sb("g01b", [P, HALF // 2, PACK], BF16)
+        interleave(nc.vector.tensor_copy, g01b, 0, raw01b, 0, HALF // 2)
+        quantise(0, 1, g01a, 0, HALF // 2)
+        quantise(0, 1, g01b, HALF // 2, HALF // 2)
+        for t in (0, 1):
+            passes(t, 0, 0)
+        for t in (0, 1):
+            passes(t, 0, 1)
+        deal(1)
+
+        empty_bank(0, 0, "slot_a")
+        empty_bank(1, 0)
+        for t in (2, 3):
+            passes(t, 0, 0)
+            passes(t, 0, 1)
+        scatter(0, 0)
+        scatter(1, 0)
+        window[2] = sb("window2", [P, T], F32, "slot_a")
+        nc.gpsimd.memset(window[2][:], 0.0)
+
+        g10 = sb("g10", [P, HALF, PACK], BF16)
+        g11 = sb("g11", [P, HALF, PACK], BF16)
+        interleave(nc.scalar.copy, g10, 0, raw10, 0, HALF)
+        interleave(nc.scalar.copy, g11, 0, raw11, 0, HALF)
+        quantise(1, 0, g10, 0, HALF)
+        quantise(1, 1, g11, 0, HALF)
+        empty_bank(2, 0, "slot_b")
+        scatter(2, 0)
+        for t in (0, 1):
+            passes(t, 1, 0)
+            passes(t, 1, 1)
+
+        out_rows = out_0.rearrange("(p t) c -> p t c", t=PACK)
+        pairs = [sb(f"pairs{c}", [P, 2, CHUNK, 2], BF16) for c in range(CHUNKS)]
+
+        def round_plane(copy, t, c):
+            copy(out=pairs[c][:, t // 2, :, t % 2], in_=window[t][:, c * CHUNK : (c + 1) * CHUNK])
+
+        empty_bank(0, 1, "slot_c")
+        passes(2, 1, 0)
+        passes(2, 1, 1)
+        empty_bank(1, 1, "slot_e")
+        scatter(0, 1)
+        nc.sync.dma_start(out=out_rows[:, 0, :], in_=window[0][:])
+        scatter(1, 1)
+        nc.sync.dma_start(out=out_rows[:, 1, :], in_=window[1][:])
+        window[3] = sb("window3", [P, T], F32, "slot_e")
+        nc.gpsimd.memset(window[3][:], 0.0)
+        empty_bank(2, 1, "slot_d")
+        empty_bank(3, 0, "slot_c")
+        passes(3, 1, 0)
+        passes(3, 1, 1)
+        for c in range(CHUNKS):
+            round_plane(nc.scalar.copy, 0, c)
+        scatter(2, 1)
+        nc.sync.dma_start(out=out_rows[:, 2, :], in_=window[2][:])
+        scatter(3, 0)
+        for t in (1, 2):
+            for c in (0, 1):
+                round_plane(nc.scalar.copy, t, c)
+        empty_bank(3, 1, "slot_d")
+        scatter(3, 1)
+        for t in (1, 2):
+            for c in (2, 3):
+                round_plane(nc.scalar.copy, t, c)
+        nc.sync.dma_start(out=out_rows[:, 3, :], in_=window[3][:])
+
+        out_scales = sb("out_scales", [P, T], U8)
+        out_words = out_1[0].rearrange("p c i -> p (c i)").bitcast(I32)
+        grouped = [sb(f"grouped{c}", [P, CHUNK, PACK], BF16) for c in range(CHUNKS)]
+        out_codes = [sb(f"out_codes{c}", [P, CHUNK], U32) for c in range(CHUNKS)]
+
+        def weave(copy, c):
+            copy(
+                out=grouped[c][:].bitcast(F32).rearrange("p (c l) u -> p c u l", l=LINE),
+                in_=pairs[c][:].rearrange("p u c e -> p u (c e)").bitcast(F32).rearrange("p u (c l) -> p c u l", l=LINE),
+            )
+
+        def finish(c):
+            cols = slice(c * CHUNK, (c + 1) * CHUNK)
+            nc.vector.quantize_mx(
+                out=out_codes[c][:].bitcast(E4M3X4),
+                scales=out_scales[:, cols],
+                in_=grouped[c][:].rearrange("p c i -> p (c i)"),
+            )
+            nc.sync.dma_start(out=out_words[:, cols], in_=out_codes[c][:].bitcast(I32))
+
+        for c in (0, 1):
+            round_plane(nc.vector.tensor_copy, 3, c)
+        for c in (0, 1):
+            weave(nc.vector.tensor_copy, c)
+        for c in (2, 3):
+            round_plane(nc.scalar.copy, 3, c)
+            weave(nc.scalar.copy, c)
+        for c in range(CHUNKS):
+            finish(c)
+        for q in range(4):
+            nc.scalar.dma_start(
+                out=out_2[0, 4 * q : 4 * q + 4, :].bitcast(I32),
+                in_=out_scales[32 * q : 32 * q + 4, :].bitcast(I32),
+            )

@@ -21,9 +21,11 @@ PACK = 4
 K_PASS = P * PACK
 PASSES = K // K_PASS
 HALF = 512
-CHUNK = 512
+QUARTER = 256
+CHUNK = 256
 CHUNKS = T // CHUNK
 LINE = 4
+VECTOR_COLS = 160
 
 
 def tile_list_embg_res_noneP_kernel(
@@ -51,53 +53,42 @@ def tile_list_embg_res_noneP_kernel(
             nc.sync.dma_start(out=raw[:], in_=rows.rearrange("(p i) j -> p i j", i=PACK))
             return raw
 
-        def load_scales(queue, dst, src):
+        def load_scales(dst, src):
             for q in range(4):
-                queue.dma_start(
+                nc.sync.dma_start(
                     out=dst[32 * q : 32 * q + 4, :, :].bitcast(I32),
                     in_=src[:, 4 * q : 4 * q + 4, :].rearrange("a r n -> r a n").bitcast(I32),
                 )
 
         raw00 = load_dy("raw00", 0, 0, HALF)
-        load_scales(nc.sync, s8_raw, w8_scales)
+        load_scales(s8_raw, w8_scales)
         w8_raw = sb("w8_raw", [P, PASSES, N], I32)
         nc.sync.dma_start(out=w8_raw[:], in_=w8_words.rearrange("a p n i -> p a (n i)").bitcast(I32))
         w4_raw = sb("w4_raw", [P, PASSES, 2 * N], U8)
         nc.sync.dma_start(out=w4_raw[:].bitcast(I32), in_=w4_words.rearrange("a p b -> p a b").bitcast(I32))
-        raw01a = load_dy("raw01a", 1, 0, HALF // 2)
-        load_scales(nc.sync, s4_raw, w4_scales)
-        raw01b = load_dy("raw01b", 1, HALF // 2, HALF // 2)
+        load_scales(s4_raw, w4_scales)
+        raw01 = [load_dy(f"raw01{q}", 1, q * QUARTER, QUARTER) for q in range(2)]
         nc.sync.dma_start(offsets[:], offs)
-        wgo_sb = [sb(f"wgo{h}", [P, HALF], F32) for h in range(2)]
-        nc.sync.dma_start(out=wgo_sb[0][:], in_=wgo[:, 0:HALF])
+        wgo_sb = sb("wgo_sb", [P, J], F32)
+        nc.sync.dma_start(out=wgo_sb[:, 0:HALF], in_=wgo[:, 0:HALF])
         raw10 = load_dy("raw10", 0, HALF, HALF)
-        raw11 = load_dy("raw11", 1, HALF, HALF, "slot_b")
-        nc.sync.dma_start(out=wgo_sb[1][:], in_=wgo[:, HALF:J])
+        raw11 = load_dy("raw11", 1, HALF, HALF, "last_raw")
+        nc.sync.dma_start(out=wgo_sb[:, HALF:J], in_=wgo[:, HALF:J])
 
         window = {}
-        for t in (0, 1):
+        for t in (2, 0):
             window[t] = sb(f"window{t}", [P, T], F32)
             nc.vector.memset(window[t][:], 0.0)
+        window[3] = window[2]
 
-        w8_t = [sb(f"w8_t{u}", [P, 2, PASSES, P], I32) for u in range(2)]
-        w4_t = [sb(f"w4_t{u}", [P, 2, PASSES, 2 * P], U8) for u in range(2)]
-        s8_t = [sb(f"s8_t{u}", [P, 2, PASSES, P], U8) for u in range(2)]
-        s4_t = [sb(f"s4_t{u}", [P, 2, PASSES, P], U8) for u in range(2)]
+        w8_t = sb("w8_t", [P, PACK, PASSES, P], I32)
+        w4_t = sb("w4_t", [P, PACK, PASSES, 2 * P], U8)
+        s8_t = sb("s8_t", [P, PACK, PASSES, P], U8)
+        s4_t = sb("s4_t", [P, PACK, PASSES, P], U8)
 
-        def deal(u):
-            ts = slice(2 * u, 2 * u + 2)
+        def deal(dealt, raw):
             nc.vector.tensor_copy(
-                out=w8_t[u][:], in_=w8_raw[:].rearrange("p a (m t) -> p t a m", t=PACK)[:, ts]
-            )
-            nc.vector.tensor_copy(
-                out=s8_t[u][:], in_=s8_raw[:].rearrange("p a (m t) -> p t a m", t=PACK)[:, ts]
-            )
-            nc.vector.tensor_copy(
-                out=w4_t[u][:].bitcast(U16),
-                in_=w4_raw[:].bitcast(U16).rearrange("p a (m t) -> p t a m", t=PACK)[:, ts],
-            )
-            nc.vector.tensor_copy(
-                out=s4_t[u][:], in_=s4_raw[:].rearrange("p a (m t) -> p t a m", t=PACK)[:, ts]
+                out=dealt.rearrange("p t a m -> p a m t"), in_=raw.rearrange("p a (m t) -> p a m t", t=PACK)
             )
 
         def interleave(copy, grouped, c0, raw, r0, width):
@@ -121,15 +112,15 @@ def tile_list_embg_res_noneP_kernel(
             )
 
         bank = {}
-        bank_tag = {(0, 0): "b0", (1, 0): "b1", (2, 0): "b0", (3, 0): "b1", (0, 1): "b2", (1, 1): "b0", (2, 1): "b2", (3, 1): "b1"}
 
         def passes(t, h, a):
             if a == 0:
-                bank[t, h] = psum.tile([P, HALF], F32, name=f"bank{t}{h}", tag=bank_tag[t, h])
+                tag = "bank21" if (t, h) == (3, 0) else f"bank{t}{h}"
+                bank[t, h] = psum.tile([P, HALF], F32, name=f"bank{t}{h}", tag=tag)
             nc.tensor.matmul_mx(
                 out=bank[t, h][:],
-                lhsT=w8_t[t // 2][:, t % 2, a, :].bitcast(E4M3X4),
-                lhsT_scale=s8_t[t // 2][:, t % 2, a, :],
+                lhsT=w8_t[:, t, a, :].bitcast(E4M3X4),
+                lhsT_scale=s8_t[:, t, a, :],
                 rhs=codes[h, a][:].bitcast(E5M2X4),
                 rhs_scale=scales[h, a][:],
                 start=(a == 0),
@@ -137,8 +128,8 @@ def tile_list_embg_res_noneP_kernel(
             )
             nc.tensor.matmul_mx(
                 out=bank[t, h][:],
-                lhsT=w4_t[t // 2][:, t % 2, a, :].bitcast(E2M1X4),
-                lhsT_scale=s4_t[t // 2][:, t % 2, a, :],
+                lhsT=w4_t[:, t, a, :].bitcast(E2M1X4),
+                lhsT_scale=s4_t[:, t, a, :],
                 rhs=codes[h, a][:].bitcast(E5M2X4),
                 rhs_scale=scales[h, a][:],
                 start=False,
@@ -154,34 +145,35 @@ def tile_list_embg_res_noneP_kernel(
         def scatter(t, h):
             cols = HALF // 16
             nc.vector.tensor_tensor(
-                window[t][:].indirect(offsets[:, h * cols : (h + 1) * cols]), dx[t, h][:], wgo_sb[h][:], MULT
+                window[t][:].indirect(offsets[:, h * cols : (h + 1) * cols]),
+                dx[t, h][:],
+                wgo_sb[:, h * HALF : (h + 1) * HALF],
+                MULT,
             )
 
-        deal(0)
+        deal(s8_t[:], s8_raw[:])
         g00 = sb("g00", [P, HALF, PACK], BF16)
-        interleave(nc.scalar.copy, g00, 0, raw00, 0, HALF)
+        interleave(nc.vector.tensor_copy, g00, 0, raw00, 0, QUARTER)
+        interleave(nc.scalar.copy, g00, QUARTER, raw00, QUARTER, QUARTER)
+        deal(w8_t[:], w8_raw[:])
         quantise(0, 0, g00, 0, HALF)
-        g01a = sb("g01a", [P, HALF // 2, PACK], BF16)
-        interleave(nc.scalar.copy, g01a, 0, raw01a, 0, HALF // 2)
-        g01b = sb("g01b", [P, HALF // 2, PACK], BF16)
-        interleave(nc.vector.tensor_copy, g01b, 0, raw01b, 0, HALF // 2)
-        quantise(0, 1, g01a, 0, HALF // 2)
-        quantise(0, 1, g01b, HALF // 2, HALF // 2)
-        for t in (0, 1):
-            passes(t, 0, 0)
-        for t in (0, 1):
-            passes(t, 0, 1)
-        deal(1)
+        deal(w4_t[:].bitcast(U16), w4_raw[:].bitcast(U16))
+        deal(s4_t[:], s4_raw[:])
+        for q in range(2):
+            g01 = sb(f"g01{q}", [P, QUARTER, PACK], BF16)
+            interleave(nc.vector.tensor_copy, g01, 0, raw01[q], 0, VECTOR_COLS)
+            interleave(nc.scalar.copy, g01, VECTOR_COLS, raw01[q], VECTOR_COLS, QUARTER - VECTOR_COLS)
+            quantise(0, 1, g01, q * QUARTER, QUARTER)
+        for a in range(PASSES):
+            for t in (2, 0, 1):
+                passes(t, 0, a)
 
-        empty_bank(0, 0, "slot_a")
-        empty_bank(1, 0)
-        for t in (2, 3):
-            passes(t, 0, 0)
-            passes(t, 0, 1)
+        empty_bank(2, 0, "first_dx")
+        empty_bank(0, 0)
+        scatter(2, 0)
         scatter(0, 0)
-        scatter(1, 0)
-        window[2] = sb("window2", [P, T], F32, "slot_a")
-        nc.gpsimd.memset(window[2][:], 0.0)
+        window[1] = sb("window1", [P, T], F32, "first_dx")
+        nc.gpsimd.memset(window[1][:], 0.0)
 
         g10 = sb("g10", [P, HALF, PACK], BF16)
         g11 = sb("g11", [P, HALF, PACK], BF16)
@@ -189,78 +181,73 @@ def tile_list_embg_res_noneP_kernel(
         interleave(nc.scalar.copy, g11, 0, raw11, 0, HALF)
         quantise(1, 0, g10, 0, HALF)
         quantise(1, 1, g11, 0, HALF)
-        empty_bank(2, 0, "slot_b")
-        scatter(2, 0)
-        for t in (0, 1):
-            passes(t, 1, 0)
-            passes(t, 1, 1)
+        empty_bank(1, 0, "last_raw")
+        scatter(1, 0)
+        for t in (2, 0, 1):
+            for a in range(PASSES):
+                passes(t, 1, a)
+            empty_bank(t, 1)
+        for h in range(2):
+            for a in range(PASSES):
+                passes(3, h, a)
+            empty_bank(3, h)
 
         out_rows = out_0.rearrange("(p t) c -> p t c", t=PACK)
-        pairs = [sb(f"pairs{c}", [P, 2, CHUNK, 2], BF16) for c in range(CHUNKS)]
+        pairs = [sb(f"pairs{c}", [P, 2, HALF, 2], BF16, f"codes{c // 2}{c % 2}") for c in range(T // HALF)]
 
-        def round_plane(copy, t, c):
-            copy(out=pairs[c][:, t // 2, :, t % 2], in_=window[t][:, c * CHUNK : (c + 1) * CHUNK])
+        def round_plane(copy, t, c0, width):
+            c, at = divmod(c0, HALF)
+            copy(out=pairs[c][:, t // 2, at : at + width, t % 2], in_=window[t][:, c0 : c0 + width])
 
-        empty_bank(0, 1, "slot_c")
-        passes(2, 1, 0)
-        passes(2, 1, 1)
-        empty_bank(1, 1, "slot_e")
-        scatter(0, 1)
-        nc.sync.dma_start(out=out_rows[:, 0, :], in_=window[0][:])
-        scatter(1, 1)
-        nc.sync.dma_start(out=out_rows[:, 1, :], in_=window[1][:])
-        window[3] = sb("window3", [P, T], F32, "slot_e")
-        nc.gpsimd.memset(window[3][:], 0.0)
-        empty_bank(2, 1, "slot_d")
-        empty_bank(3, 0, "slot_c")
-        passes(3, 1, 0)
-        passes(3, 1, 1)
-        for c in range(CHUNKS):
-            round_plane(nc.scalar.copy, 0, c)
-        scatter(2, 1)
-        nc.sync.dma_start(out=out_rows[:, 2, :], in_=window[2][:])
+        for t in (2, 0, 1):
+            scatter(t, 1)
+            nc.sync.dma_start(out=out_rows[:, t, :], in_=window[t][:])
+            for c0 in range(0, T, HALF):
+                round_plane(nc.scalar.copy, t, c0, HALF)
         scatter(3, 0)
-        for t in (1, 2):
-            for c in (0, 1):
-                round_plane(nc.scalar.copy, t, c)
-        empty_bank(3, 1, "slot_d")
         scatter(3, 1)
-        for t in (1, 2):
-            for c in (2, 3):
-                round_plane(nc.scalar.copy, t, c)
         nc.sync.dma_start(out=out_rows[:, 3, :], in_=window[3][:])
 
         out_scales = sb("out_scales", [P, T], U8)
         out_words = out_1[0].rearrange("p c i -> p (c i)").bitcast(I32)
         grouped = [sb(f"grouped{c}", [P, CHUNK, PACK], BF16) for c in range(CHUNKS)]
-        out_codes = [sb(f"out_codes{c}", [P, CHUNK], U32) for c in range(CHUNKS)]
+        out_codes = [sb(f"out_codes{c}", [P, HALF], U32) for c in range(T // HALF)]
 
-        def weave(copy, c):
+        def weave(copy, k):
+            c, at = divmod(k * CHUNK, HALF)
+            words = pairs[c][:].rearrange("p u c e -> p u (c e)").bitcast(F32)[:, :, at : at + CHUNK]
             copy(
-                out=grouped[c][:].bitcast(F32).rearrange("p (c l) u -> p c u l", l=LINE),
-                in_=pairs[c][:].rearrange("p u c e -> p u (c e)").bitcast(F32).rearrange("p u (c l) -> p c u l", l=LINE),
+                out=grouped[k][:].bitcast(F32).rearrange("p (c l) u -> p c u l", l=LINE),
+                in_=words.rearrange("p u (c l) -> p c u l", l=LINE),
             )
 
-        def finish(c):
-            cols = slice(c * CHUNK, (c + 1) * CHUNK)
+        def finish(k):
+            c, at = divmod(k * CHUNK, HALF)
             nc.vector.quantize_mx(
-                out=out_codes[c][:].bitcast(E4M3X4),
-                scales=out_scales[:, cols],
-                in_=grouped[c][:].rearrange("p c i -> p (c i)"),
+                out=out_codes[c][:, at : at + CHUNK].bitcast(E4M3X4),
+                scales=out_scales[:, k * CHUNK : (k + 1) * CHUNK],
+                in_=grouped[k][:].rearrange("p c i -> p (c i)"),
             )
-            nc.sync.dma_start(out=out_words[:, cols], in_=out_codes[c][:].bitcast(I32))
 
-        for c in (0, 1):
-            round_plane(nc.vector.tensor_copy, 3, c)
-        for c in (0, 1):
-            weave(nc.vector.tensor_copy, c)
-        for c in (2, 3):
-            round_plane(nc.scalar.copy, 3, c)
-            weave(nc.scalar.copy, c)
-        for c in range(CHUNKS):
-            finish(c)
-        for q in range(4):
-            nc.scalar.dma_start(
-                out=out_2[0, 4 * q : 4 * q + 4, :].bitcast(I32),
-                in_=out_scales[32 * q : 32 * q + 4, :].bitcast(I32),
-            )
+        def store_codes(c):
+            nc.sync.dma_start(out=out_words[:, c * HALF : (c + 1) * HALF], in_=out_codes[c][:].bitcast(I32))
+
+        def store_scales(queue, c0, width):
+            for q in range(4):
+                queue.dma_start(
+                    out=out_2[0, 4 * q : 4 * q + 4, c0 : c0 + width].bitcast(I32),
+                    in_=out_scales[32 * q : 32 * q + 4, c0 : c0 + width].bitcast(I32),
+                )
+
+        for c0 in (0, HALF):
+            round_plane(nc.vector.tensor_copy, 3, c0, HALF)
+        for k in range(CHUNKS // 2):
+            weave(nc.vector.tensor_copy, k)
+        for k in range(CHUNKS // 2, CHUNKS):
+            round_plane(nc.scalar.copy, 3, k * CHUNK, CHUNK)
+            weave(nc.scalar.copy, k)
+        for k in range(CHUNKS):
+            finish(k)
+            if k % 2 == 1:
+                store_codes(k // 2)
+        store_scales(nc.scalar, 0, T)

@@ -26,6 +26,7 @@ CHUNK = 256
 CHUNKS = T // CHUNK
 LINE = 4
 VECTOR_COLS = 160
+ODD = T // 2 - 1
 
 
 def tile_list_embg_res_noneP_kernel(
@@ -44,8 +45,8 @@ def tile_list_embg_res_noneP_kernel(
 
         s8_raw = sb("s8_raw", [P, PASSES, N], U8)
         s4_raw = sb("s4_raw", [P, PASSES, N], U8)
-        nc.vector.memset(s8_raw[:].rearrange("p a n -> p (a n)").bitcast(I32), 0)
-        nc.vector.memset(s4_raw[:].rearrange("p a n -> p (a n)").bitcast(I32), 0)
+        nc.gpsimd.memset(s8_raw[:].rearrange("p a n -> p (a n)").bitcast(I32), 0)
+        nc.gpsimd.memset(s4_raw[:].rearrange("p a n -> p (a n)").bitcast(I32), 0)
 
         def load_dy(name, a, j0, width, tag=None):
             raw = sb(name, [P, PACK, width], F32, tag)
@@ -64,10 +65,10 @@ def tile_list_embg_res_noneP_kernel(
         load_scales(s8_raw, w8_scales)
         w8_raw = sb("w8_raw", [P, PASSES, N], I32)
         nc.sync.dma_start(out=w8_raw[:], in_=w8_words.rearrange("a p n i -> p a (n i)").bitcast(I32))
-        w4_raw = sb("w4_raw", [P, PASSES, 2 * N], U8)
-        nc.sync.dma_start(out=w4_raw[:].bitcast(I32), in_=w4_words.rearrange("a p b -> p a b").bitcast(I32))
         load_scales(s4_raw, w4_scales)
         raw01 = [load_dy(f"raw01{q}", 1, q * QUARTER, QUARTER) for q in range(2)]
+        w4_raw = sb("w4_raw", [P, PASSES, 2 * N], U8)
+        nc.sync.dma_start(out=w4_raw[:].bitcast(I32), in_=w4_words.rearrange("a p b -> p a b").bitcast(I32))
         nc.sync.dma_start(offsets[:], offs)
         wgo_sb = sb("wgo_sb", [P, J], F32)
         nc.sync.dma_start(out=wgo_sb[:, 0:HALF], in_=wgo[:, 0:HALF])
@@ -78,11 +79,13 @@ def tile_list_embg_res_noneP_kernel(
         window = {}
         for t in (2, 0):
             window[t] = sb(f"window{t}", [P, T], F32)
-            nc.vector.memset(window[t][:], 0.0)
+        nc.vector.memset(window[2][:, 0:ODD], 0.0)
+        nc.vector.memset(window[2][:, ODD:T], 0.0)
+        nc.gpsimd.memset(window[0][:], 0.0)
         window[3] = window[2]
 
         w8_t = sb("w8_t", [P, PACK, PASSES, P], I32)
-        w4_t = sb("w4_t", [P, PACK, PASSES, 2 * P], U8)
+        w4_t = [sb(f"w4_t{t}", [P, PASSES, 2 * P], U8) for t in range(PACK)]
         s8_t = sb("s8_t", [P, PACK, PASSES, P], U8)
         s4_t = sb("s4_t", [P, PACK, PASSES, P], U8)
 
@@ -113,28 +116,29 @@ def tile_list_embg_res_noneP_kernel(
 
         bank = {}
 
-        def passes(t, h, a):
-            if a == 0:
-                tag = "bank21" if (t, h) == (3, 0) else f"bank{t}{h}"
-                bank[t, h] = psum.tile([P, HALF], F32, name=f"bank{t}{h}", tag=tag)
-            nc.tensor.matmul_mx(
-                out=bank[t, h][:],
-                lhsT=w8_t[:, t, a, :].bitcast(E4M3X4),
-                lhsT_scale=s8_t[:, t, a, :],
-                rhs=codes[h, a][:].bitcast(E5M2X4),
-                rhs_scale=scales[h, a][:],
-                start=(a == 0),
-                stop=False,
-            )
-            nc.tensor.matmul_mx(
-                out=bank[t, h][:],
-                lhsT=w4_t[:, t, a, :].bitcast(E2M1X4),
-                lhsT_scale=s4_t[:, t, a, :],
-                rhs=codes[h, a][:].bitcast(E5M2X4),
-                rhs_scale=scales[h, a][:],
-                start=False,
-                stop=(a == PASSES - 1),
-            )
+        def passes(t, h):
+            tag = "bank21" if (t, h) == (3, 0) else f"bank{t}{h}"
+            bank[t, h] = psum.tile([P, HALF], F32, name=f"bank{t}{h}", tag=tag)
+            for a in range(PASSES):
+                nc.tensor.matmul_mx(
+                    out=bank[t, h][:],
+                    lhsT=w8_t[:, t, a, :].bitcast(E4M3X4),
+                    lhsT_scale=s8_t[:, t, a, :],
+                    rhs=codes[h, a][:].bitcast(E5M2X4),
+                    rhs_scale=scales[h, a][:],
+                    start=(a == 0),
+                    stop=False,
+                )
+            for a in range(PASSES):
+                nc.tensor.matmul_mx(
+                    out=bank[t, h][:],
+                    lhsT=w4_t[t][:, a, :].bitcast(E2M1X4),
+                    lhsT_scale=s4_t[:, t, a, :],
+                    rhs=codes[h, a][:].bitcast(E5M2X4),
+                    rhs_scale=scales[h, a][:],
+                    start=False,
+                    stop=(a == PASSES - 1),
+                )
 
         dx = {}
 
@@ -151,22 +155,25 @@ def tile_list_embg_res_noneP_kernel(
                 MULT,
             )
 
-        deal(s8_t[:], s8_raw[:])
         g00 = sb("g00", [P, HALF, PACK], BF16)
         interleave(nc.vector.tensor_copy, g00, 0, raw00, 0, QUARTER)
         interleave(nc.scalar.copy, g00, QUARTER, raw00, QUARTER, QUARTER)
-        deal(w8_t[:], w8_raw[:])
+        deal(s8_t[:], s8_raw[:])
         quantise(0, 0, g00, 0, HALF)
-        deal(w4_t[:].bitcast(U16), w4_raw[:].bitcast(U16))
+        deal(w8_t[:], w8_raw[:])
         deal(s4_t[:], s4_raw[:])
+        g01 = [sb(f"g01{q}", [P, QUARTER, PACK], BF16) for q in range(2)]
+        interleave(nc.scalar.copy, g01[0], 0, raw01[0], 0, QUARTER)
+        interleave(nc.vector.tensor_copy, g01[1], 0, raw01[1], 0, VECTOR_COLS)
+        interleave(nc.scalar.copy, g01[1], VECTOR_COLS, raw01[1], VECTOR_COLS, QUARTER - VECTOR_COLS)
         for q in range(2):
-            g01 = sb(f"g01{q}", [P, QUARTER, PACK], BF16)
-            interleave(nc.vector.tensor_copy, g01, 0, raw01[q], 0, VECTOR_COLS)
-            interleave(nc.scalar.copy, g01, VECTOR_COLS, raw01[q], VECTOR_COLS, QUARTER - VECTOR_COLS)
-            quantise(0, 1, g01, q * QUARTER, QUARTER)
-        for a in range(PASSES):
-            for t in (2, 0, 1):
-                passes(t, 0, a)
+            quantise(0, 1, g01[q], q * QUARTER, QUARTER)
+        for t in (2, 0, 1, 3):
+            nc.vector.tensor_copy(
+                out=w4_t[t][:].bitcast(U16), in_=w4_raw[:].bitcast(U16).rearrange("p a (m t) -> p t a m", t=PACK)[:, t]
+            )
+        for t in (2, 0, 1):
+            passes(t, 0)
 
         empty_bank(2, 0, "first_dx")
         empty_bank(0, 0)
@@ -184,13 +191,12 @@ def tile_list_embg_res_noneP_kernel(
         empty_bank(1, 0, "last_raw")
         scatter(1, 0)
         for t in (2, 0, 1):
-            for a in range(PASSES):
-                passes(t, 1, a)
+            passes(t, 1)
             empty_bank(t, 1)
+        dx3 = sb("dx3", [P, J], F32)
         for h in range(2):
-            for a in range(PASSES):
-                passes(3, h, a)
-            empty_bank(3, h)
+            passes(3, h)
+            nc.scalar.copy(out=dx3[:, h * HALF : (h + 1) * HALF], in_=bank[3, h][:])
 
         out_rows = out_0.rearrange("(p t) c -> p t c", t=PACK)
         pairs = [sb(f"pairs{c}", [P, 2, HALF, 2], BF16, f"codes{c // 2}{c % 2}") for c in range(T // HALF)]
@@ -204,11 +210,10 @@ def tile_list_embg_res_noneP_kernel(
             nc.sync.dma_start(out=out_rows[:, t, :], in_=window[t][:])
             for c0 in range(0, T, HALF):
                 round_plane(nc.scalar.copy, t, c0, HALF)
-        scatter(3, 0)
-        scatter(3, 1)
+        nc.vector.tensor_tensor(window[3][:].indirect(offsets[:]), dx3[:], wgo_sb[:], MULT)
         nc.sync.dma_start(out=out_rows[:, 3, :], in_=window[3][:])
 
-        out_scales = sb("out_scales", [P, T], U8)
+        out_scales = sb("out_scales", [P, HALF], U8)
         out_words = out_1[0].rearrange("p c i -> p (c i)").bitcast(I32)
         grouped = [sb(f"grouped{c}", [P, CHUNK, PACK], BF16) for c in range(CHUNKS)]
         out_codes = [sb(f"out_codes{c}", [P, HALF], U32) for c in range(T // HALF)]
@@ -225,19 +230,14 @@ def tile_list_embg_res_noneP_kernel(
             c, at = divmod(k * CHUNK, HALF)
             nc.vector.quantize_mx(
                 out=out_codes[c][:, at : at + CHUNK].bitcast(E4M3X4),
-                scales=out_scales[:, k * CHUNK : (k + 1) * CHUNK],
+                scales=out_scales[4 * c : P, at : at + CHUNK],
                 in_=grouped[k][:].rearrange("p c i -> p (c i)"),
             )
 
-        def store_codes(c):
-            nc.sync.dma_start(out=out_words[:, c * HALF : (c + 1) * HALF], in_=out_codes[c][:].bitcast(I32))
-
-        def store_scales(queue, c0, width):
-            for q in range(4):
-                queue.dma_start(
-                    out=out_2[0, 4 * q : 4 * q + 4, c0 : c0 + width].bitcast(I32),
-                    in_=out_scales[32 * q : 32 * q + 4, c0 : c0 + width].bitcast(I32),
-                )
+        def store_codes(c, at, width):
+            nc.sync.dma_start(
+                out=out_words[:, c * HALF + at : c * HALF + at + width], in_=out_codes[c][:, at : at + width].bitcast(I32)
+            )
 
         for c0 in (0, HALF):
             round_plane(nc.vector.tensor_copy, 3, c0, HALF)
@@ -248,6 +248,12 @@ def tile_list_embg_res_noneP_kernel(
             weave(nc.scalar.copy, k)
         for k in range(CHUNKS):
             finish(k)
-            if k % 2 == 1:
-                store_codes(k // 2)
-        store_scales(nc.scalar, 0, T)
+            if k >= CHUNKS - 2:
+                store_codes(k // 2, (k % 2) * CHUNK, CHUNK)
+            elif k % 2 == 1:
+                store_codes(k // 2, 0, HALF)
+        for q in range(4):
+            nc.scalar.dma_start(
+                out=out_2[0, 4 * q : 4 * q + 4, :].bitcast(I32).rearrange("r (c w) -> c r w", c=T // HALF),
+                in_=out_scales[32 * q : 32 * q + 16, :].bitcast(I32),
+            )

@@ -27,6 +27,7 @@ CHUNKS = T // CHUNK
 LINE = 4
 VECTOR_COLS = 160
 ODD = T // 2 - 1
+FIRST, SECOND, THIRD, LAST = 0, 2, 3, 1
 
 
 def tile_list_embg_res_noneP_kernel(
@@ -65,8 +66,9 @@ def tile_list_embg_res_noneP_kernel(
         load_scales(s8_raw, w8_scales)
         w8_raw = sb("w8_raw", [P, PASSES, N], I32)
         nc.sync.dma_start(out=w8_raw[:], in_=w8_words.rearrange("a p n i -> p a (n i)").bitcast(I32))
+        raw01 = [load_dy("raw010", 1, 0, QUARTER)]
         load_scales(s4_raw, w4_scales)
-        raw01 = [load_dy(f"raw01{q}", 1, q * QUARTER, QUARTER) for q in range(2)]
+        raw01.append(load_dy("raw011", 1, QUARTER, QUARTER))
         w4_raw = sb("w4_raw", [P, PASSES, 2 * N], U8)
         nc.sync.dma_start(out=w4_raw[:].bitcast(I32), in_=w4_words.rearrange("a p b -> p a b").bitcast(I32))
         nc.sync.dma_start(offsets[:], offs)
@@ -77,22 +79,17 @@ def tile_list_embg_res_noneP_kernel(
         nc.sync.dma_start(out=wgo_sb[:, HALF:J], in_=wgo[:, HALF:J])
 
         window = {}
-        for t in (2, 0):
+        for t in (FIRST, SECOND):
             window[t] = sb(f"window{t}", [P, T], F32)
-        nc.vector.memset(window[2][:, 0:ODD], 0.0)
-        nc.vector.memset(window[2][:, ODD:T], 0.0)
-        nc.gpsimd.memset(window[0][:], 0.0)
-        window[3] = window[2]
+        nc.vector.memset(window[FIRST][:, 0:ODD], 0.0)
+        nc.vector.memset(window[FIRST][:, ODD:T], 0.0)
+        nc.gpsimd.memset(window[SECOND][:], 0.0)
+        window[LAST] = window[FIRST]
 
         w8_t = sb("w8_t", [P, PACK, PASSES, P], I32)
-        w4_t = [sb(f"w4_t{t}", [P, PASSES, 2 * P], U8) for t in range(PACK)]
         s8_t = sb("s8_t", [P, PACK, PASSES, P], U8)
-        s4_t = sb("s4_t", [P, PACK, PASSES, P], U8)
-
-        def deal(dealt, raw):
-            nc.vector.tensor_copy(
-                out=dealt.rearrange("p t a m -> p a m t"), in_=raw.rearrange("p a (m t) -> p a m t", t=PACK)
-            )
+        w4_t = {}
+        s4_t = {}
 
         def interleave(copy, grouped, c0, raw, r0, width):
             copy(
@@ -117,7 +114,7 @@ def tile_list_embg_res_noneP_kernel(
         bank = {}
 
         def passes(t, h):
-            tag = "bank21" if (t, h) == (3, 0) else f"bank{t}{h}"
+            tag = "second_half" if h == 1 else f"bank{FIRST if t == LAST else t}"
             bank[t, h] = psum.tile([P, HALF], F32, name=f"bank{t}{h}", tag=tag)
             for a in range(PASSES):
                 nc.tensor.matmul_mx(
@@ -129,11 +126,10 @@ def tile_list_embg_res_noneP_kernel(
                     start=(a == 0),
                     stop=False,
                 )
-            for a in range(PASSES):
                 nc.tensor.matmul_mx(
                     out=bank[t, h][:],
-                    lhsT=w4_t[t][:, a, :].bitcast(E2M1X4),
-                    lhsT_scale=s4_t[:, t, a, :],
+                    lhsT=w4_t[t, a].bitcast(E2M1X4),
+                    lhsT_scale=s4_t[t, a],
                     rhs=codes[h, a][:].bitcast(E5M2X4),
                     rhs_scale=scales[h, a][:],
                     start=False,
@@ -158,29 +154,45 @@ def tile_list_embg_res_noneP_kernel(
         g00 = sb("g00", [P, HALF, PACK], BF16)
         interleave(nc.vector.tensor_copy, g00, 0, raw00, 0, QUARTER)
         interleave(nc.scalar.copy, g00, QUARTER, raw00, QUARTER, QUARTER)
-        deal(s8_t[:], s8_raw[:])
+        nc.vector.tensor_copy(out=s8_t[:], in_=s8_raw[:].rearrange("p a (m t) -> p t a m", t=PACK))
         quantise(0, 0, g00, 0, HALF)
-        deal(w8_t[:], w8_raw[:])
-        deal(s4_t[:], s4_raw[:])
+        nc.vector.tensor_copy(
+            out=w8_t[:].rearrange("p t a m -> p a m t"), in_=w8_raw[:].rearrange("p a (m t) -> p a m t", t=PACK)
+        )
         g01 = [sb(f"g01{q}", [P, QUARTER, PACK], BF16) for q in range(2)]
-        interleave(nc.scalar.copy, g01[0], 0, raw01[0], 0, QUARTER)
-        interleave(nc.vector.tensor_copy, g01[1], 0, raw01[1], 0, VECTOR_COLS)
-        interleave(nc.scalar.copy, g01[1], VECTOR_COLS, raw01[1], VECTOR_COLS, QUARTER - VECTOR_COLS)
-        for q in range(2):
-            quantise(0, 1, g01[q], q * QUARTER, QUARTER)
-        for t in (2, 0, 1, 3):
+
+        def deal_w4(t0, count, tag=None):
+            ts = slice(t0, t0 + count)
+            size = PASSES * count * P
+            both = sb(f"w4_t{t0}", [P, 3 * size], U8, tag)
+            words = both[:, 0 : 2 * size].rearrange("p (a t b) -> p a t b", a=PASSES, t=count)
+            scale_bytes = both[:, 2 * size : 3 * size].rearrange("p (a t m) -> p a t m", a=PASSES, t=count)
+            nc.vector.tensor_copy(out=scale_bytes, in_=s4_raw[:].rearrange("p a (m t) -> p a t m", t=PACK)[:, :, ts])
             nc.vector.tensor_copy(
-                out=w4_t[t][:].bitcast(U16), in_=w4_raw[:].bitcast(U16).rearrange("p a (m t) -> p t a m", t=PACK)[:, t]
+                out=words.bitcast(U16), in_=w4_raw[:].bitcast(U16).rearrange("p a (m t) -> p a t m", t=PACK)[:, :, ts]
             )
-        for t in (2, 0, 1):
+            for t in range(count):
+                for a in range(PASSES):
+                    s4_t[t0 + t, a] = scale_bytes[:, a, t, :]
+                    w4_t[t0 + t, a] = words[:, a, t, :]
+
+        for q in range(2):
+            interleave(nc.vector.tensor_copy, g01[q], 0, raw01[q], 0, VECTOR_COLS)
+            interleave(nc.scalar.copy, g01[q], VECTOR_COLS, raw01[q], VECTOR_COLS, QUARTER - VECTOR_COLS)
+            if q == 1:
+                deal_w4(FIRST, 1)
+            quantise(0, 1, g01[q], q * QUARTER, QUARTER)
+        deal_w4(FIRST + 1, PACK - 1, "g011")
+        for t in (FIRST, SECOND, THIRD):
             passes(t, 0)
 
-        empty_bank(2, 0, "first_dx")
-        empty_bank(0, 0)
-        scatter(2, 0)
-        scatter(0, 0)
-        window[1] = sb("window1", [P, T], F32, "first_dx")
-        nc.gpsimd.memset(window[1][:], 0.0)
+        empty_bank(FIRST, 0, "first_dx")
+        passes(LAST, 0)
+        empty_bank(SECOND, 0)
+        scatter(FIRST, 0)
+        scatter(SECOND, 0)
+        window[THIRD] = sb("third_window", [P, T], F32, "first_dx")
+        nc.gpsimd.memset(window[THIRD][:], 0.0)
 
         g10 = sb("g10", [P, HALF, PACK], BF16)
         g11 = sb("g11", [P, HALF, PACK], BF16)
@@ -188,30 +200,31 @@ def tile_list_embg_res_noneP_kernel(
         interleave(nc.scalar.copy, g11, 0, raw11, 0, HALF)
         quantise(1, 0, g10, 0, HALF)
         quantise(1, 1, g11, 0, HALF)
-        empty_bank(1, 0, "last_raw")
-        scatter(1, 0)
-        for t in (2, 0, 1):
+        empty_bank(THIRD, 0, "last_raw")
+        scatter(THIRD, 0)
+        for t in (FIRST, SECOND, THIRD):
             passes(t, 1)
             empty_bank(t, 1)
-        dx3 = sb("dx3", [P, J], F32)
-        for h in range(2):
-            passes(3, h)
-            nc.scalar.copy(out=dx3[:, h * HALF : (h + 1) * HALF], in_=bank[3, h][:])
+            if t == FIRST:
+                dx_last = sb("dx_last", [P, J], F32, "g11")
+                nc.scalar.copy(out=dx_last[:, 0:HALF], in_=bank[LAST, 0][:])
+        passes(LAST, 1)
+        nc.scalar.copy(out=dx_last[:, HALF:J], in_=bank[LAST, 1][:])
 
         out_rows = out_0.rearrange("(p t) c -> p t c", t=PACK)
-        pairs = [sb(f"pairs{c}", [P, 2, HALF, 2], BF16, f"codes{c // 2}{c % 2}") for c in range(T // HALF)]
+        pairs = [sb(f"pairs{c}", [P, 2, HALF, 2], BF16, ("codes1", "scales1")[c // 2] + str(c % 2)) for c in range(T // HALF)]
 
         def round_plane(copy, t, c0, width):
             c, at = divmod(c0, HALF)
             copy(out=pairs[c][:, t // 2, at : at + width, t % 2], in_=window[t][:, c0 : c0 + width])
 
-        for t in (2, 0, 1):
+        for t in (FIRST, SECOND, THIRD):
             scatter(t, 1)
             nc.sync.dma_start(out=out_rows[:, t, :], in_=window[t][:])
             for c0 in range(0, T, HALF):
                 round_plane(nc.scalar.copy, t, c0, HALF)
-        nc.vector.tensor_tensor(window[3][:].indirect(offsets[:]), dx3[:], wgo_sb[:], MULT)
-        nc.sync.dma_start(out=out_rows[:, 3, :], in_=window[3][:])
+        nc.vector.tensor_tensor(window[LAST][:].indirect(offsets[:]), dx_last[:], wgo_sb[:], MULT)
+        nc.sync.dma_start(out=out_rows[:, LAST, :], in_=window[LAST][:])
 
         out_scales = sb("out_scales", [P, HALF], U8)
         out_words = out_1[0].rearrange("p c i -> p (c i)").bitcast(I32)
@@ -240,11 +253,11 @@ def tile_list_embg_res_noneP_kernel(
             )
 
         for c0 in (0, HALF):
-            round_plane(nc.vector.tensor_copy, 3, c0, HALF)
+            round_plane(nc.vector.tensor_copy, LAST, c0, HALF)
         for k in range(CHUNKS // 2):
             weave(nc.vector.tensor_copy, k)
         for k in range(CHUNKS // 2, CHUNKS):
-            round_plane(nc.scalar.copy, 3, k * CHUNK, CHUNK)
+            round_plane(nc.scalar.copy, LAST, k * CHUNK, CHUNK)
             weave(nc.scalar.copy, k)
         for k in range(CHUNKS):
             finish(k)

@@ -27,6 +27,7 @@ CHUNKS = T // CHUNK
 LINE = 4
 VECTOR_COLS = 160
 ODD = T // 2 - 1
+WARM_UPS = 2
 FIRST, SECOND, THIRD, LAST = 0, 2, 3, 1
 
 
@@ -156,6 +157,17 @@ def tile_list_embg_res_noneP_kernel(
         interleave(nc.scalar.copy, g00, QUARTER, raw00, QUARTER, QUARTER)
         nc.vector.tensor_copy(out=s8_t[:], in_=s8_raw[:].rearrange("p a (m t) -> p t a m", t=PACK))
         quantise(0, 0, g00, 0, HALF)
+        warm = psum.tile([P, HALF], F32, name="warm")
+        for step in range(WARM_UPS):
+            nc.tensor.matmul_mx(
+                out=warm[:],
+                lhsT=w8_raw[:, 0, 0:P].bitcast(E4M3X4),
+                lhsT_scale=s8_raw[:, 0, 0:P],
+                rhs=codes[0, 0][:].bitcast(E5M2X4),
+                rhs_scale=scales[0, 0][:],
+                start=True,
+                stop=True,
+            )
         nc.vector.tensor_copy(
             out=w8_t[:].rearrange("p t a m -> p a m t"), in_=w8_raw[:].rearrange("p a (m t) -> p a m t", t=PACK)
         )

@@ -21,14 +21,14 @@ PACK = 4
 K_PASS = P * PACK
 PASSES = K // K_PASS
 HALF = 512
-QUARTER = 256
+PIECE = 256
 CHUNK = 256
 CHUNKS = T // CHUNK
 LINE = 4
-VECTOR_COLS = 160
+VECTOR_COLS = 128
 ODD = T // 2 - 1
-WARM_UPS = 2
 FIRST, SECOND, THIRD, LAST = 0, 2, 3, 1
+A, B, C, D = range(4)
 
 
 def tile_list_embg_res_noneP_kernel(
@@ -45,16 +45,17 @@ def tile_list_embg_res_noneP_kernel(
 
         offsets = listp.tile([P, J // 16], U16, name="offsets")
 
-        s8_raw = sb("s8_raw", [P, PASSES, N], U8)
         s4_raw = sb("s4_raw", [P, PASSES, N], U8)
-        nc.gpsimd.memset(s8_raw[:].rearrange("p a n -> p (a n)").bitcast(I32), 0)
+        s8_raw = sb("s8_raw", [P, PASSES, N], U8)
         nc.gpsimd.memset(s4_raw[:].rearrange("p a n -> p (a n)").bitcast(I32), 0)
+        nc.gpsimd.memset(s8_raw[:].rearrange("p a n -> p (a n)").bitcast(I32), 0)
 
-        def load_dy(name, a, j0, width, tag=None):
-            raw = sb(name, [P, PACK, width], F32, tag)
-            rows = dy[a * K_PASS : (a + 1) * K_PASS, j0 : j0 + width]
-            nc.sync.dma_start(out=raw[:], in_=rows.rearrange("(p i) j -> p i j", i=PACK))
-            return raw
+        raw = {}
+
+        def load_dy(piece, a):
+            raw[piece, a] = sb(f"raw{piece}{a}", [P, PACK, PIECE], F32)
+            rows = dy[a * K_PASS : (a + 1) * K_PASS, piece * PIECE : (piece + 1) * PIECE]
+            nc.sync.dma_start(out=raw[piece, a][:], in_=rows.rearrange("(p i) j -> p i j", i=PACK))
 
         def load_scales(dst, src):
             for q in range(4):
@@ -63,21 +64,23 @@ def tile_list_embg_res_noneP_kernel(
                     in_=src[:, 4 * q : 4 * q + 4, :].rearrange("a r n -> r a n").bitcast(I32),
                 )
 
-        raw00 = load_dy("raw00", 0, 0, HALF)
-        load_scales(s8_raw, w8_scales)
-        w8_raw = sb("w8_raw", [P, PASSES, N], I32)
-        nc.sync.dma_start(out=w8_raw[:], in_=w8_words.rearrange("a p n i -> p a (n i)").bitcast(I32))
-        raw01 = [load_dy("raw010", 1, 0, QUARTER)]
-        load_scales(s4_raw, w4_scales)
-        raw01.append(load_dy("raw011", 1, QUARTER, QUARTER))
+        load_dy(A, 0)
+        nc.sync.dma_start(offsets[:], offs)
         w4_raw = sb("w4_raw", [P, PASSES, 2 * N], U8)
         nc.sync.dma_start(out=w4_raw[:].bitcast(I32), in_=w4_words.rearrange("a p b -> p a b").bitcast(I32))
-        nc.sync.dma_start(offsets[:], offs)
+        load_scales(s4_raw, w4_scales)
+        load_dy(A, 1)
+        w8_raw = sb("w8_raw", [P, PASSES, N], I32)
+        nc.sync.dma_start(out=w8_raw[:], in_=w8_words.rearrange("a p n i -> p a (n i)").bitcast(I32))
+        load_scales(s8_raw, w8_scales)
         wgo_sb = sb("wgo_sb", [P, J], F32)
-        nc.sync.dma_start(out=wgo_sb[:, 0:HALF], in_=wgo[:, 0:HALF])
-        raw10 = load_dy("raw10", 0, HALF, HALF)
-        raw11 = load_dy("raw11", 1, HALF, HALF, "last_raw")
-        nc.sync.dma_start(out=wgo_sb[:, HALF:J], in_=wgo[:, HALF:J])
+        nc.sync.dma_start(out=wgo_sb[:, 0:PIECE], in_=wgo[:, 0:PIECE])
+        for piece in (B, C):
+            for a in range(PASSES):
+                load_dy(piece, a)
+        nc.sync.dma_start(out=wgo_sb[:, PIECE:J], in_=wgo[:, PIECE:J])
+        for a in range(PASSES):
+            load_dy(D, a)
 
         window = {}
         for t in (FIRST, SECOND):
@@ -87,15 +90,14 @@ def tile_list_embg_res_noneP_kernel(
         nc.gpsimd.memset(window[SECOND][:], 0.0)
         window[LAST] = window[FIRST]
 
-        w8_t = sb("w8_t", [P, PACK, PASSES, P], I32)
-        s8_t = sb("s8_t", [P, PACK, PASSES, P], U8)
-        w4_t = {}
-        s4_t = {}
+        grouped_dy = {}
 
-        def interleave(copy, grouped, c0, raw, r0, width):
+        def interleave(copy, piece, a, c0, width):
+            if c0 == 0:
+                grouped_dy[piece, a] = sb(f"g{piece}{a}", [P, PIECE, PACK], BF16)
             copy(
-                out=grouped[:, c0 : c0 + width, :].rearrange("p (c l) i -> p c i l", l=LINE),
-                in_=raw[:, :, r0 : r0 + width].rearrange("p i (c l) -> p c i l", l=LINE),
+                out=grouped_dy[piece, a][:, c0 : c0 + width, :].rearrange("p (c l) i -> p c i l", l=LINE),
+                in_=raw[piece, a][:, :, c0 : c0 + width].rearrange("p i (c l) -> p c i l", l=LINE),
             )
 
         codes = {}
@@ -105,123 +107,130 @@ def tile_list_embg_res_noneP_kernel(
                 codes[h, a] = sb(f"codes{h}{a}", [P, HALF], U32)
                 scales[h, a] = sb(f"scales{h}{a}", [P, HALF], U8)
 
-        def quantise(h, a, grouped, c0, width):
+        def quantise(piece, a):
+            h, c0 = divmod(piece * PIECE, HALF)
             nc.vector.quantize_mx(
-                out=codes[h, a][:, c0 : c0 + width].bitcast(E5M2X4),
-                scales=scales[h, a][:, c0 : c0 + width],
-                in_=grouped[:].rearrange("p c i -> p (c i)"),
+                out=codes[h, a][:, c0 : c0 + PIECE].bitcast(E5M2X4),
+                scales=scales[h, a][:, c0 : c0 + PIECE],
+                in_=grouped_dy[piece, a][:].rearrange("p c i -> p (c i)"),
             )
+
+        w4_t = sb("w4_t", [P, PACK, PASSES, 2 * P], U8)
+        s4_t = sb("s4_t", [P, PACK, PASSES, P], U8)
+        w8_first = sb("w8_first", [P, 1, PASSES, P], U32)
+        s8_first = sb("s8_first", [P, 1, PASSES, P], U8)
+        w8_rest = sb("w8_rest", [P, PACK - 1, PASSES, P], U32)
+        s8_rest = sb("s8_rest", [P, PACK - 1, PASSES, P], U8)
+
+        def w8_slice(first, rest, t, a):
+            return first[:, 0, a, :] if t == FIRST else rest[:, t - 1, a, :]
 
         bank = {}
 
-        def passes(t, h):
-            tag = "second_half" if h == 1 else f"bank{FIRST if t == LAST else t}"
-            bank[t, h] = psum.tile([P, HALF], F32, name=f"bank{t}{h}", tag=tag)
-            for a in range(PASSES):
+        def product(t, piece, width, tag, order=((4, 0), (4, 1), (8, 0), (8, 1))):
+            h, c0 = divmod(piece * PIECE, HALF)
+            cols = slice(c0, c0 + width)
+            bank[t, piece] = psum.tile([P, width], F32, name=f"bank{t}{piece}", tag=tag)
+            for step, (bits, a) in enumerate(order):
+                if bits == 4:
+                    words, bytes_of_scale = w4_t[:, t, a, :].bitcast(E2M1X4), s4_t[:, t, a, :]
+                else:
+                    words = w8_slice(w8_first, w8_rest, t, a).bitcast(E4M3X4)
+                    bytes_of_scale = w8_slice(s8_first, s8_rest, t, a)
                 nc.tensor.matmul_mx(
-                    out=bank[t, h][:],
-                    lhsT=w8_t[:, t, a, :].bitcast(E4M3X4),
-                    lhsT_scale=s8_t[:, t, a, :],
-                    rhs=codes[h, a][:].bitcast(E5M2X4),
-                    rhs_scale=scales[h, a][:],
-                    start=(a == 0),
-                    stop=False,
-                )
-                nc.tensor.matmul_mx(
-                    out=bank[t, h][:],
-                    lhsT=w4_t[t, a].bitcast(E2M1X4),
-                    lhsT_scale=s4_t[t, a],
-                    rhs=codes[h, a][:].bitcast(E5M2X4),
-                    rhs_scale=scales[h, a][:],
-                    start=False,
-                    stop=(a == PASSES - 1),
+                    out=bank[t, piece][:],
+                    lhsT=words,
+                    lhsT_scale=bytes_of_scale,
+                    rhs=codes[h, a][:, cols].bitcast(E5M2X4),
+                    rhs_scale=scales[h, a][:, cols],
+                    start=(step == 0),
+                    stop=(step == len(order) - 1),
                 )
 
         dx = {}
 
-        def empty_bank(t, h, tag=None):
-            dx[t, h] = sb(f"dx{t}{h}", [P, HALF], F32, tag)
-            nc.scalar.copy(out=dx[t, h][:], in_=bank[t, h][:])
+        def empty_bank(copy, t, piece, dst):
+            dx[t, piece] = dst
+            copy(out=dst, in_=bank[t, piece][:])
 
-        def scatter(t, h):
-            cols = HALF // 16
+        def scatter(t, piece, width):
+            j0 = piece * PIECE
             nc.vector.tensor_tensor(
-                window[t][:].indirect(offsets[:, h * cols : (h + 1) * cols]),
-                dx[t, h][:],
-                wgo_sb[:, h * HALF : (h + 1) * HALF],
+                window[t][:].indirect(offsets[:, j0 // 16 : (j0 + width) // 16]),
+                dx[t, piece],
+                wgo_sb[:, j0 : j0 + width],
                 MULT,
             )
 
-        g00 = sb("g00", [P, HALF, PACK], BF16)
-        interleave(nc.vector.tensor_copy, g00, 0, raw00, 0, QUARTER)
-        interleave(nc.scalar.copy, g00, QUARTER, raw00, QUARTER, QUARTER)
-        nc.vector.tensor_copy(out=s8_t[:], in_=s8_raw[:].rearrange("p a (m t) -> p t a m", t=PACK))
-        quantise(0, 0, g00, 0, HALF)
-        warm = psum.tile([P, HALF], F32, name="warm")
-        for step in range(WARM_UPS):
-            nc.tensor.matmul_mx(
-                out=warm[:],
-                lhsT=w8_raw[:, 0, 0:P].bitcast(E4M3X4),
-                lhsT_scale=s8_raw[:, 0, 0:P],
-                rhs=codes[0, 0][:].bitcast(E5M2X4),
-                rhs_scale=scales[0, 0][:],
-                start=True,
-                stop=True,
-            )
-        nc.vector.tensor_copy(
-            out=w8_t[:].rearrange("p t a m -> p a m t"), in_=w8_raw[:].rearrange("p a (m t) -> p a m t", t=PACK)
+        nc.scalar.copy(
+            out=w4_t[:].bitcast(U16).rearrange("p t a m -> p a m t"),
+            in_=w4_raw[:].bitcast(U16).rearrange("p a (m t) -> p a m t", t=PACK),
         )
-        g01 = [sb(f"g01{q}", [P, QUARTER, PACK], BF16) for q in range(2)]
-
-        def deal_w4(t0, count, tag=None):
-            ts = slice(t0, t0 + count)
-            size = PASSES * count * P
-            both = sb(f"w4_t{t0}", [P, 3 * size], U8, tag)
-            words = both[:, 0 : 2 * size].rearrange("p (a t b) -> p a t b", a=PASSES, t=count)
-            scale_bytes = both[:, 2 * size : 3 * size].rearrange("p (a t m) -> p a t m", a=PASSES, t=count)
-            nc.vector.tensor_copy(out=scale_bytes, in_=s4_raw[:].rearrange("p a (m t) -> p a t m", t=PACK)[:, :, ts])
-            nc.vector.tensor_copy(
-                out=words.bitcast(U16), in_=w4_raw[:].bitcast(U16).rearrange("p a (m t) -> p a t m", t=PACK)[:, :, ts]
-            )
-            for t in range(count):
-                for a in range(PASSES):
-                    s4_t[t0 + t, a] = scale_bytes[:, a, t, :]
-                    w4_t[t0 + t, a] = words[:, a, t, :]
-
-        for q in range(2):
-            interleave(nc.vector.tensor_copy, g01[q], 0, raw01[q], 0, VECTOR_COLS)
-            interleave(nc.scalar.copy, g01[q], VECTOR_COLS, raw01[q], VECTOR_COLS, QUARTER - VECTOR_COLS)
-            if q == 1:
-                deal_w4(FIRST, 1)
-            quantise(0, 1, g01[q], q * QUARTER, QUARTER)
-        deal_w4(FIRST + 1, PACK - 1, "g011")
-        for t in (FIRST, SECOND, THIRD):
-            passes(t, 0)
-
-        empty_bank(FIRST, 0, "first_dx")
-        passes(LAST, 0)
-        empty_bank(SECOND, 0)
-        scatter(FIRST, 0)
-        scatter(SECOND, 0)
-        window[THIRD] = sb("third_window", [P, T], F32, "first_dx")
+        interleave(nc.vector.tensor_copy, A, 0, 0, PIECE)
+        quantise(A, 0)
+        nc.vector.tensor_copy(out=s4_t[:], in_=s4_raw[:].rearrange("p a (m t) -> p t a m", t=PACK))
+        interleave(nc.vector.tensor_copy, A, 1, 0, VECTOR_COLS)
+        interleave(nc.scalar.copy, A, 1, VECTOR_COLS, PIECE - VECTOR_COLS)
+        quantise(A, 1)
+        w8_by_slice = w8_raw[:].bitcast(U32).rearrange("p a (m t) -> p a m t", t=PACK)
+        s8_by_slice = s8_raw[:].rearrange("p a (m t) -> p t a m", t=PACK)
+        nc.vector.tensor_copy(
+            out=w8_first[:].bitcast(I32), in_=w8_raw[:].rearrange("p a (m t) -> p t a m", t=PACK)[:, 0:1]
+        )
+        nc.scalar.copy(out=w8_rest[:].rearrange("p t a m -> p a m t"), in_=w8_by_slice[:, :, :, 1:PACK])
+        nc.vector.tensor_copy(out=s8_first[:], in_=s8_by_slice[:, 0:1])
+        nc.vector.tensor_copy(
+            out=s8_rest[:].rearrange("p t a m -> p a t m"),
+            in_=s8_raw[:].rearrange("p a (m t) -> p a t m", t=PACK)[:, :, 1:PACK],
+        )
+        window[THIRD] = sb("third_window", [P, T], F32, "s8_raw")
         nc.gpsimd.memset(window[THIRD][:], 0.0)
 
-        g10 = sb("g10", [P, HALF, PACK], BF16)
-        g11 = sb("g11", [P, HALF, PACK], BF16)
-        interleave(nc.scalar.copy, g10, 0, raw10, 0, HALF)
-        interleave(nc.scalar.copy, g11, 0, raw11, 0, HALF)
-        quantise(1, 0, g10, 0, HALF)
-        quantise(1, 1, g11, 0, HALF)
-        empty_bank(THIRD, 0, "last_raw")
-        scatter(THIRD, 0)
-        for t in (FIRST, SECOND, THIRD):
-            passes(t, 1)
-            empty_bank(t, 1)
-            if t == FIRST:
-                dx_last = sb("dx_last", [P, J], F32, "g11")
-                nc.scalar.copy(out=dx_last[:, 0:HALF], in_=bank[LAST, 0][:])
-        passes(LAST, 1)
-        nc.scalar.copy(out=dx_last[:, HALF:J], in_=bank[LAST, 1][:])
+        product(FIRST, A, PIECE, "bank0")
+        for n, t in enumerate((SECOND, THIRD)):
+            product(t, A, PIECE, f"bank{1 + n}", ((4, 0), (8, 0), (8, 1), (4, 1)))
+        empty_bank(nc.vector.tensor_copy, FIRST, A, sb("dx_fa", [P, PIECE], F32)[:])
+        scatter(FIRST, A, PIECE)
+        interleave(nc.scalar.copy, B, 0, 0, PIECE)
+        quantise(B, 0)
+        empty_bank(nc.scalar.copy, SECOND, A, sb("dx_sa", [P, PIECE], F32, f"raw{B}0")[:])
+        scatter(SECOND, A, PIECE)
+        interleave(nc.scalar.copy, B, 1, 0, PIECE)
+        quantise(B, 1)
+        empty_bank(nc.scalar.copy, THIRD, A, sb("dx_ta", [P, PIECE], F32, f"raw{B}1")[:])
+        scatter(THIRD, A, PIECE)
+        for n, t in enumerate((FIRST, SECOND, THIRD)):
+            product(t, B, PIECE, f"bank{3 + n}")
+        product(LAST, A, HALF, "bank0")
+
+        for a in range(PASSES):
+            interleave(nc.scalar.copy, C, a, 0, PIECE)
+            quantise(C, a)
+        empty_bank(nc.scalar.copy, FIRST, B, sb("dx_fb", [P, PIECE], F32, f"raw{C}1")[:])
+        scatter(FIRST, B, PIECE)
+        product(FIRST, C, PIECE, "bank6")
+
+        interleave(nc.scalar.copy, D, 0, 0, PIECE)
+        quantise(D, 0)
+        empty_bank(nc.scalar.copy, SECOND, B, sb("dx_sb", [P, PIECE], F32, f"raw{D}0")[:])
+        scatter(SECOND, B, PIECE)
+        interleave(nc.scalar.copy, D, 1, 0, PIECE)
+        quantise(D, 1)
+        held = sb("dx_held", [P, 2, PIECE], F32, f"raw{D}1")
+        empty_bank(nc.scalar.copy, FIRST, C, held[:, 0, :])
+        scatter(FIRST, C, PIECE)
+        empty_bank(nc.scalar.copy, THIRD, B, held[:, 1, :])
+        scatter(THIRD, B, PIECE)
+
+        dx_last = sb("dx_last", [P, J], F32, f"g{D}1")
+        empty_bank(nc.scalar.copy, LAST, A, dx_last[:, 0:HALF])
+        product(FIRST, D, PIECE, "bank7")
+        empty_bank(nc.scalar.copy, FIRST, D, sb("dx_fd", [P, PIECE], F32)[:])
+        for n, t in enumerate((SECOND, THIRD)):
+            product(t, C, HALF, f"bank{1 + n}")
+            empty_bank(nc.scalar.copy, t, C, sb(f"dx_c{t}", [P, HALF], F32)[:])
+        product(LAST, C, HALF, "bank3")
+        empty_bank(nc.scalar.copy, LAST, C, dx_last[:, HALF:J])
 
         out_rows = out_0.rearrange("(p t) c -> p t c", t=PACK)
         pairs = [sb(f"pairs{c}", [P, 2, HALF, 2], BF16, ("codes1", "scales1")[c // 2] + str(c % 2)) for c in range(T // HALF)]
@@ -230,8 +239,8 @@ def tile_list_embg_res_noneP_kernel(
             c, at = divmod(c0, HALF)
             copy(out=pairs[c][:, t // 2, at : at + width, t % 2], in_=window[t][:, c0 : c0 + width])
 
-        for t in (FIRST, SECOND, THIRD):
-            scatter(t, 1)
+        for t, piece, width in ((FIRST, D, PIECE), (SECOND, C, HALF), (THIRD, C, HALF)):
+            scatter(t, piece, width)
             nc.sync.dma_start(out=out_rows[:, t, :], in_=window[t][:])
             for c0 in range(0, T, HALF):
                 round_plane(nc.scalar.copy, t, c0, HALF)

@@ -75,12 +75,13 @@ def tile_list_embg_res_noneP_kernel(
         load_scales(s8_raw, w8_scales)
         wgo_sb = sb("wgo_sb", [P, J], F32)
         nc.sync.dma_start(out=wgo_sb[:, 0:PIECE], in_=wgo[:, 0:PIECE])
-        for piece in (B, C):
-            for a in range(PASSES):
-                load_dy(piece, a)
-        nc.sync.dma_start(out=wgo_sb[:, PIECE:J], in_=wgo[:, PIECE:J])
         for a in range(PASSES):
-            load_dy(D, a)
+            load_dy(B, a)
+        nc.sync.dma_start(out=wgo_sb[:, PIECE:HALF], in_=wgo[:, PIECE:HALF])
+        for a in range(PASSES):
+            for piece in (C, D):
+                load_dy(piece, a)
+        nc.sync.dma_start(out=wgo_sb[:, HALF:J], in_=wgo[:, HALF:J])
 
         window = {}
         for t in (FIRST, SECOND):
@@ -93,10 +94,12 @@ def tile_list_embg_res_noneP_kernel(
         grouped_dy = {}
 
         def interleave(copy, piece, a, c0, width):
-            if c0 == 0:
-                grouped_dy[piece, a] = sb(f"g{piece}{a}", [P, PIECE, PACK], BF16)
+            first = min(piece, C)
+            if (first, a) not in grouped_dy:
+                grouped_dy[first, a] = sb(f"g{first}{a}", [P, HALF if first == C else PIECE, PACK], BF16)
+            at = (piece - first) * PIECE + c0
             copy(
-                out=grouped_dy[piece, a][:, c0 : c0 + width, :].rearrange("p (c l) i -> p c i l", l=LINE),
+                out=grouped_dy[first, a][:, at : at + width, :].rearrange("p (c l) i -> p c i l", l=LINE),
                 in_=raw[piece, a][:, :, c0 : c0 + width].rearrange("p i (c l) -> p c i l", l=LINE),
             )
 
@@ -107,11 +110,11 @@ def tile_list_embg_res_noneP_kernel(
                 codes[h, a] = sb(f"codes{h}{a}", [P, HALF], U32)
                 scales[h, a] = sb(f"scales{h}{a}", [P, HALF], U8)
 
-        def quantise(piece, a):
+        def quantise(piece, a, width):
             h, c0 = divmod(piece * PIECE, HALF)
             nc.vector.quantize_mx(
-                out=codes[h, a][:, c0 : c0 + PIECE].bitcast(E5M2X4),
-                scales=scales[h, a][:, c0 : c0 + PIECE],
+                out=codes[h, a][:, c0 : c0 + width].bitcast(E5M2X4),
+                scales=scales[h, a][:, c0 : c0 + width],
                 in_=grouped_dy[piece, a][:].rearrange("p c i -> p (c i)"),
             )
 
@@ -127,10 +130,10 @@ def tile_list_embg_res_noneP_kernel(
 
         bank = {}
 
-        def product(t, piece, width, tag, order=((4, 0), (4, 1), (8, 0), (8, 1))):
+        def product(t, piece, width, tag, order=((4, 0), (8, 0), (4, 1), (8, 1)), into=None):
             h, c0 = divmod(piece * PIECE, HALF)
             cols = slice(c0, c0 + width)
-            bank[t, piece] = psum.tile([P, width], F32, name=f"bank{t}{piece}", tag=tag)
+            bank[t, piece] = into if tag is None else psum.tile([P, width], F32, name=f"bank{t}{piece}", tag=tag)
             for step, (bits, a) in enumerate(order):
                 if bits == 4:
                     words, bytes_of_scale = w4_t[:, t, a, :].bitcast(E2M1X4), s4_t[:, t, a, :]
@@ -167,11 +170,11 @@ def tile_list_embg_res_noneP_kernel(
             in_=w4_raw[:].bitcast(U16).rearrange("p a (m t) -> p a m t", t=PACK),
         )
         interleave(nc.vector.tensor_copy, A, 0, 0, PIECE)
-        quantise(A, 0)
+        quantise(A, 0, PIECE)
         nc.vector.tensor_copy(out=s4_t[:], in_=s4_raw[:].rearrange("p a (m t) -> p t a m", t=PACK))
         interleave(nc.vector.tensor_copy, A, 1, 0, VECTOR_COLS)
         interleave(nc.scalar.copy, A, 1, VECTOR_COLS, PIECE - VECTOR_COLS)
-        quantise(A, 1)
+        quantise(A, 1, PIECE)
         w8_by_slice = w8_raw[:].bitcast(U32).rearrange("p a (m t) -> p a m t", t=PACK)
         s8_by_slice = s8_raw[:].rearrange("p a (m t) -> p t a m", t=PACK)
         nc.vector.tensor_copy(
@@ -186,48 +189,44 @@ def tile_list_embg_res_noneP_kernel(
         window[THIRD] = sb("third_window", [P, T], F32, "s8_raw")
         nc.gpsimd.memset(window[THIRD][:], 0.0)
 
-        product(FIRST, A, PIECE, "bank0")
+        product(FIRST, A, PIECE, "bank0", ((4, 0), (4, 1), (8, 0), (8, 1)))
         for n, t in enumerate((SECOND, THIRD)):
             product(t, A, PIECE, f"bank{1 + n}", ((4, 0), (8, 0), (8, 1), (4, 1)))
         empty_bank(nc.vector.tensor_copy, FIRST, A, sb("dx_fa", [P, PIECE], F32)[:])
         scatter(FIRST, A, PIECE)
-        interleave(nc.scalar.copy, B, 0, 0, PIECE)
-        quantise(B, 0)
-        empty_bank(nc.scalar.copy, SECOND, A, sb("dx_sa", [P, PIECE], F32, f"raw{B}0")[:])
-        scatter(SECOND, A, PIECE)
-        interleave(nc.scalar.copy, B, 1, 0, PIECE)
-        quantise(B, 1)
-        empty_bank(nc.scalar.copy, THIRD, A, sb("dx_ta", [P, PIECE], F32, f"raw{B}1")[:])
-        scatter(THIRD, A, PIECE)
-        for n, t in enumerate((FIRST, SECOND, THIRD)):
-            product(t, B, PIECE, f"bank{3 + n}")
-        product(LAST, A, HALF, "bank0")
-
         for a in range(PASSES):
-            interleave(nc.scalar.copy, C, a, 0, PIECE)
-            quantise(C, a)
-        empty_bank(nc.scalar.copy, FIRST, B, sb("dx_fb", [P, PIECE], F32, f"raw{C}1")[:])
-        scatter(FIRST, B, PIECE)
-        product(FIRST, C, PIECE, "bank6")
+            interleave(nc.scalar.copy, B, a, 0, PIECE)
+            quantise(B, a, PIECE)
+        early = sb("dx_early", [P, PIECE + HALF], F32, f"raw{B}1")
+        empty_bank(nc.scalar.copy, SECOND, A, early[:, 0:PIECE])
+        scatter(SECOND, A, PIECE)
+        dx_third = early[:, PIECE : PIECE + HALF]
+        empty_bank(nc.scalar.copy, THIRD, A, dx_third[:, 0:PIECE])
+        product(THIRD, B, PIECE, "bank3")
+        interleave(nc.scalar.copy, C, 0, 0, PIECE)
+        empty_bank(nc.scalar.copy, THIRD, B, dx_third[:, PIECE:HALF])
+        dx[THIRD, A] = dx_third
+        scatter(THIRD, A, HALF)
 
         interleave(nc.scalar.copy, D, 0, 0, PIECE)
-        quantise(D, 0)
-        empty_bank(nc.scalar.copy, SECOND, B, sb("dx_sb", [P, PIECE], F32, f"raw{D}0")[:])
-        scatter(SECOND, B, PIECE)
+        quantise(C, 0, HALF)
+        interleave(nc.scalar.copy, C, 1, 0, PIECE)
         interleave(nc.scalar.copy, D, 1, 0, PIECE)
-        quantise(D, 1)
+        quantise(C, 1, HALF)
         held = sb("dx_held", [P, 2, PIECE], F32, f"raw{D}1")
-        empty_bank(nc.scalar.copy, FIRST, C, held[:, 0, :])
-        scatter(FIRST, C, PIECE)
-        empty_bank(nc.scalar.copy, THIRD, B, held[:, 1, :])
-        scatter(THIRD, B, PIECE)
-
-        dx_last = sb("dx_last", [P, J], F32, f"g{D}1")
+        both = psum.tile([P, 2, HALF], F32, name="both", tag="bank3")
+        for n, t in enumerate((FIRST, SECOND)):
+            product(t, B, PIECE, None, into=both[:, 0, n * PIECE : (n + 1) * PIECE])
+        product(LAST, A, HALF, None, into=both[:, 1, :])
+        nc.scalar.copy(out=held[:].rearrange("p n c -> p (n c)"), in_=both[:, 0, :])
+        dx_last = sb("dx_last", [P, J], F32, f"g{C}1")
         empty_bank(nc.scalar.copy, LAST, A, dx_last[:, 0:HALF])
-        product(FIRST, D, PIECE, "bank7")
-        empty_bank(nc.scalar.copy, FIRST, D, sb("dx_fd", [P, PIECE], F32)[:])
-        for n, t in enumerate((SECOND, THIRD)):
-            product(t, C, HALF, f"bank{1 + n}")
+        for n, t in enumerate((FIRST, SECOND)):
+            dx[t, B] = held[:, n, :]
+            scatter(t, B, PIECE)
+
+        for n, t in enumerate((FIRST, SECOND, THIRD)):
+            product(t, C, HALF, ("bank4", "bank3")[n % 2])
             empty_bank(nc.scalar.copy, t, C, sb(f"dx_c{t}", [P, HALF], F32)[:])
         product(LAST, C, HALF, "bank3")
         empty_bank(nc.scalar.copy, LAST, C, dx_last[:, HALF:J])
@@ -239,8 +238,8 @@ def tile_list_embg_res_noneP_kernel(
             c, at = divmod(c0, HALF)
             copy(out=pairs[c][:, t // 2, at : at + width, t % 2], in_=window[t][:, c0 : c0 + width])
 
-        for t, piece, width in ((FIRST, D, PIECE), (SECOND, C, HALF), (THIRD, C, HALF)):
-            scatter(t, piece, width)
+        for t in (FIRST, SECOND, THIRD):
+            scatter(t, C, HALF)
             nc.sync.dma_start(out=out_rows[:, t, :], in_=window[t][:])
             for c0 in range(0, T, HALF):
                 round_plane(nc.scalar.copy, t, c0, HALF)

@@ -281,9 +281,7 @@ def tile_list_embg_res_noneP_kernel(
             weave(nc.scalar.copy, k)
         for k in range(CHUNKS):
             finish(k)
-            if k >= CHUNKS - 2:
-                store_codes(k // 2, (k % 2) * CHUNK, CHUNK)
-            elif k % 2 == 1:
+            if k % 2 == 1:
                 store_codes(k // 2, 0, HALF)
         for q in range(4):
             nc.scalar.dma_start(

@@ -29,6 +29,7 @@ VECTOR_COLS = 128
 ODD = T // 2 - 1
 FIRST, SECOND, THIRD, LAST = 0, 2, 3, 1
 A, B, C, D = range(4)
+BY_K = ((4, 0), (8, 0), (4, 1), (8, 1))
 
 
 def tile_list_embg_res_noneP_kernel(
@@ -112,10 +113,12 @@ def tile_list_embg_res_noneP_kernel(
 
         def quantise(piece, a, width):
             h, c0 = divmod(piece * PIECE, HALF)
+            first = min(piece, C)
+            at = (piece - first) * PIECE
             nc.vector.quantize_mx(
                 out=codes[h, a][:, c0 : c0 + width].bitcast(E5M2X4),
                 scales=scales[h, a][:, c0 : c0 + width],
-                in_=grouped_dy[piece, a][:].rearrange("p c i -> p (c i)"),
+                in_=grouped_dy[first, a][:, at : at + width, :].rearrange("p c i -> p (c i)"),
             )
 
         w4_t = sb("w4_t", [P, PACK, PASSES, 2 * P], U8)
@@ -130,7 +133,7 @@ def tile_list_embg_res_noneP_kernel(
 
         bank = {}
 
-        def product(t, piece, width, tag, order=((4, 0), (8, 0), (4, 1), (8, 1)), into=None):
+        def product(t, piece, width, tag, order=BY_K, into=None, opens=True, closes=True):
             h, c0 = divmod(piece * PIECE, HALF)
             cols = slice(c0, c0 + width)
             bank[t, piece] = into if tag is None else psum.tile([P, width], F32, name=f"bank{t}{piece}", tag=tag)
@@ -146,8 +149,8 @@ def tile_list_embg_res_noneP_kernel(
                     lhsT_scale=bytes_of_scale,
                     rhs=codes[h, a][:, cols].bitcast(E5M2X4),
                     rhs_scale=scales[h, a][:, cols],
-                    start=(step == 0),
-                    stop=(step == len(order) - 1),
+                    start=(opens and step == 0),
+                    stop=(closes and step == len(order) - 1),
                 )
 
         dx = {}
@@ -197,38 +200,43 @@ def tile_list_embg_res_noneP_kernel(
         for a in range(PASSES):
             interleave(nc.scalar.copy, B, a, 0, PIECE)
             quantise(B, a, PIECE)
-        early = sb("dx_early", [P, PIECE + HALF], F32, f"raw{B}1")
-        empty_bank(nc.scalar.copy, SECOND, A, early[:, 0:PIECE])
-        scatter(SECOND, A, PIECE)
-        dx_third = early[:, PIECE : PIECE + HALF]
-        empty_bank(nc.scalar.copy, THIRD, A, dx_third[:, 0:PIECE])
-        product(THIRD, B, PIECE, "bank3")
+        early = sb("dx_early", [P, 2, PIECE], F32, f"raw{B}1")
+        for n, t in enumerate((SECOND, THIRD)):
+            empty_bank(nc.scalar.copy, t, A, early[:, n, :])
+            scatter(t, A, PIECE)
+        product(FIRST, B, PIECE, "bank3")
         interleave(nc.scalar.copy, C, 0, 0, PIECE)
-        empty_bank(nc.scalar.copy, THIRD, B, dx_third[:, PIECE:HALF])
-        dx[THIRD, A] = dx_third
-        scatter(THIRD, A, HALF)
-
         interleave(nc.scalar.copy, D, 0, 0, PIECE)
         quantise(C, 0, HALF)
-        interleave(nc.scalar.copy, C, 1, 0, PIECE)
-        interleave(nc.scalar.copy, D, 1, 0, PIECE)
-        quantise(C, 1, HALF)
-        held = sb("dx_held", [P, 2, PIECE], F32, f"raw{D}1")
-        both = psum.tile([P, 2, HALF], F32, name="both", tag="bank3")
-        for n, t in enumerate((FIRST, SECOND)):
+        empty_bank(nc.scalar.copy, FIRST, B, sb("dx_fb", [P, PIECE], F32, f"raw{D}0")[:])
+        scatter(FIRST, B, PIECE)
+
+        both = psum.tile([P, 2, HALF], F32, name="both", tag="bank0")
+        for n, t in enumerate((THIRD, SECOND)):
             product(t, B, PIECE, None, into=both[:, 0, n * PIECE : (n + 1) * PIECE])
         product(LAST, A, HALF, None, into=both[:, 1, :])
-        nc.scalar.copy(out=held[:].rearrange("p n c -> p (n c)"), in_=both[:, 0, :])
+        product(FIRST, C, HALF, "bank4", BY_K[:2], closes=False)
+        first_late = bank[FIRST, C]
+        for piece in (C, D):
+            interleave(nc.scalar.copy, piece, 1, 0, PIECE)
+            quantise(piece, 1, PIECE)
+            at = (piece - C) * PIECE
+            product(FIRST, piece, PIECE, None, BY_K[2:], first_late[:, at : at + PIECE], False, piece == D)
+        bank[FIRST, C] = first_late
+        held = sb("dx_held", [P, 4, PIECE], F32, f"raw{D}1")
+        nc.scalar.copy(out=held[:, 0:2, :].rearrange("p n c -> p (n c)"), in_=both[:, 0, :])
         dx_last = sb("dx_last", [P, J], F32, f"g{C}1")
         empty_bank(nc.scalar.copy, LAST, A, dx_last[:, 0:HALF])
-        for n, t in enumerate((FIRST, SECOND)):
-            dx[t, B] = held[:, n, :]
-            scatter(t, B, PIECE)
+        dx[THIRD, B] = held[:, 0, :]
+        scatter(THIRD, B, PIECE)
 
-        for n, t in enumerate((FIRST, SECOND, THIRD)):
-            product(t, C, HALF, ("bank4", "bank3")[n % 2])
-            empty_bank(nc.scalar.copy, t, C, sb(f"dx_c{t}", [P, HALF], F32)[:])
-        product(LAST, C, HALF, "bank3")
+        empty_bank(nc.scalar.copy, FIRST, C, sb("dx_first_late", [P, HALF], F32)[:])
+        product(THIRD, C, HALF, "bank0")
+        empty_bank(nc.scalar.copy, THIRD, C, sb("dx_third_late", [P, HALF], F32)[:])
+        product(SECOND, C, HALF, "bank4")
+        empty_bank(nc.scalar.copy, SECOND, C, held[:, 2:4, :].rearrange("p n c -> p (n c)"))
+        dx[SECOND, B] = held[:, 1:4, :].rearrange("p n c -> p (n c)")
+        product(LAST, C, HALF, "bank0")
         empty_bank(nc.scalar.copy, LAST, C, dx_last[:, HALF:J])
 
         out_rows = out_0.rearrange("(p t) c -> p t c", t=PACK)
@@ -238,8 +246,8 @@ def tile_list_embg_res_noneP_kernel(
             c, at = divmod(c0, HALF)
             copy(out=pairs[c][:, t // 2, at : at + width, t % 2], in_=window[t][:, c0 : c0 + width])
 
-        for t in (FIRST, SECOND, THIRD):
-            scatter(t, C, HALF)
+        for t, piece in ((FIRST, C), (THIRD, C), (SECOND, B)):
+            scatter(t, piece, J - piece * PIECE)
             nc.sync.dma_start(out=out_rows[:, t, :], in_=window[t][:])
             for c0 in range(0, T, HALF):
                 round_plane(nc.scalar.copy, t, c0, HALF)

@@ -27,6 +27,7 @@ CHUNKS = T // CHUNK
 LINE = 4
 VECTOR_COLS = 128
 ODD = T // 2 - 1
+VECTOR_TAIL = 896
 FIRST, SECOND, THIRD, LAST = 0, 2, 3, 1
 A, B, C, D = range(4)
 BY_K = ((4, 0), (8, 0), (4, 1), (8, 1))
@@ -242,30 +243,50 @@ def tile_list_embg_res_noneP_kernel(
         out_rows = out_0.rearrange("(p t) c -> p t c", t=PACK)
         pairs = [sb(f"pairs{c}", [P, 2, HALF, 2], BF16, ("codes1", "scales1")[c // 2] + str(c % 2)) for c in range(T // HALF)]
 
-        def round_plane(copy, t, c0, width):
+        grouped = [sb(f"grouped{c}", [P, CHUNK, PACK], BF16) for c in range(CHUNKS)]
+
+        def runs(c0, c1, size):
+            edges = [c0] + list(range((c0 // size + 1) * size, c1, size)) + [c1]
+            return list(zip(edges[:-1], edges[1:]))
+
+        def round_plane(copy, t, c0, c1):
             c, at = divmod(c0, HALF)
-            copy(out=pairs[c][:, t // 2, at : at + width, t % 2], in_=window[t][:, c0 : c0 + width])
+            copy(out=pairs[c][:, t // 2, at : at + c1 - c0, t % 2], in_=window[t][:, c0:c1])
+
+        def round_into_both_halves(t, c0, c1):
+            c, at = divmod(c0, HALF)
+            nc.scalar.copy(
+                out=pairs[c][:, t // 2, at : at + c1 - c0, :],
+                in_=window[t][:, c0:c1].unsqueeze(2).to_broadcast([P, c1 - c0, 2]),
+            )
+
+        def weave(copy, c0, c1):
+            c, at = divmod(c0, HALF)
+            k, to = divmod(c0, CHUNK)
+            words = pairs[c][:].rearrange("p u c e -> p u (c e)").bitcast(F32)[:, :, at : at + c1 - c0]
+            copy(
+                out=grouped[k][:].bitcast(F32)[:, to : to + c1 - c0, :].rearrange("p (c l) u -> p c u l", l=LINE),
+                in_=words.rearrange("p u (c l) -> p c u l", l=LINE),
+            )
 
         for t, piece in ((FIRST, C), (THIRD, C), (SECOND, B)):
             scatter(t, piece, J - piece * PIECE)
             nc.sync.dma_start(out=out_rows[:, t, :], in_=window[t][:])
-            for c0 in range(0, T, HALF):
-                round_plane(nc.scalar.copy, t, c0, HALF)
+            for c0, c1 in runs(0, VECTOR_TAIL, HALF):
+                round_plane(nc.scalar.copy, t, c0, c1)
+            for c0, c1 in runs(VECTOR_TAIL, T, HALF):
+                if t == FIRST:
+                    round_into_both_halves(t, c0, c1)
+                else:
+                    round_plane(nc.scalar.copy, t, c0, c1)
+        for c0, c1 in runs(VECTOR_TAIL, T, CHUNK):
+            weave(nc.scalar.copy, c0, c1)
         nc.vector.tensor_tensor(window[LAST][:].indirect(offsets[:]), dx_last[:], wgo_sb[:], MULT)
         nc.sync.dma_start(out=out_rows[:, LAST, :], in_=window[LAST][:])
 
         out_scales = sb("out_scales", [P, HALF], U8)
         out_words = out_1[0].rearrange("p c i -> p (c i)").bitcast(I32)
-        grouped = [sb(f"grouped{c}", [P, CHUNK, PACK], BF16) for c in range(CHUNKS)]
         out_codes = [sb(f"out_codes{c}", [P, HALF], U32) for c in range(T // HALF)]
-
-        def weave(copy, k):
-            c, at = divmod(k * CHUNK, HALF)
-            words = pairs[c][:].rearrange("p u c e -> p u (c e)").bitcast(F32)[:, :, at : at + CHUNK]
-            copy(
-                out=grouped[k][:].bitcast(F32).rearrange("p (c l) u -> p c u l", l=LINE),
-                in_=words.rearrange("p u (c l) -> p c u l", l=LINE),
-            )
 
         def finish(k):
             c, at = divmod(k * CHUNK, HALF)
@@ -275,22 +296,18 @@ def tile_list_embg_res_noneP_kernel(
                 in_=grouped[k][:].rearrange("p c i -> p (c i)"),
             )
 
-        def store_codes(c, at, width):
-            nc.sync.dma_start(
-                out=out_words[:, c * HALF + at : c * HALF + at + width], in_=out_codes[c][:, at : at + width].bitcast(I32)
-            )
-
-        for c0 in (0, HALF):
-            round_plane(nc.vector.tensor_copy, LAST, c0, HALF)
-        for k in range(CHUNKS // 2):
-            weave(nc.vector.tensor_copy, k)
-        for k in range(CHUNKS // 2, CHUNKS):
-            round_plane(nc.scalar.copy, LAST, k * CHUNK, CHUNK)
-            weave(nc.scalar.copy, k)
+        for c0, c1 in runs(0, VECTOR_TAIL, HALF):
+            round_plane(nc.vector.tensor_copy, LAST, c0, c1)
+        for c0, c1 in runs(0, VECTOR_TAIL, CHUNK):
+            weave(nc.vector.tensor_copy, c0, c1)
+        for c0, c1 in runs(VECTOR_TAIL, T, CHUNK):
+            k, to = divmod(c0, CHUNK)
+            nc.scalar.copy(out=grouped[k][:, to : to + c1 - c0, LAST], in_=window[LAST][:, c0:c1])
         for k in range(CHUNKS):
             finish(k)
             if k % 2 == 1:
-                store_codes(k // 2, 0, HALF)
+                c = k // 2
+                nc.sync.dma_start(out=out_words[:, c * HALF : (c + 1) * HALF], in_=out_codes[c][:].bitcast(I32))
         for q in range(4):
             nc.scalar.dma_start(
                 out=out_2[0, 4 * q : 4 * q + 4, :].bitcast(I32).rearrange("r (c w) -> c r w", c=T // HALF),

@@ -198,12 +198,10 @@ def tile_list_embg_res_noneP_kernel(
             product(t, A, PIECE, f"bank{1 + n}", ((4, 0), (8, 0), (8, 1), (4, 1)))
         empty_bank(nc.vector.tensor_copy, FIRST, A, sb("dx_fa", [P, PIECE], F32)[:])
         scatter(FIRST, A, PIECE)
-        for a in range(PASSES):
+        for a, (t, tag) in enumerate(((SECOND, None), (THIRD, f"raw{B}0"))):
             interleave(nc.scalar.copy, B, a, 0, PIECE)
             quantise(B, a, PIECE)
-        early = sb("dx_early", [P, 2, PIECE], F32, f"raw{B}1")
-        for n, t in enumerate((SECOND, THIRD)):
-            empty_bank(nc.scalar.copy, t, A, early[:, n, :])
+            empty_bank(nc.scalar.copy, t, A, sb(f"dx_early{t}", [P, PIECE], F32, tag)[:])
             scatter(t, A, PIECE)
         product(FIRST, B, PIECE, "bank3")
         interleave(nc.scalar.copy, C, 0, 0, PIECE)
@@ -219,7 +217,8 @@ def tile_list_embg_res_noneP_kernel(
         product(FIRST, C, HALF, "bank4", BY_K[:2], closes=False)
         first_late = bank[FIRST, C]
         for piece in (C, D):
-            interleave(nc.scalar.copy, piece, 1, 0, PIECE)
+            for c0, c1 in ((0, PIECE // 2), (PIECE // 2, PIECE)) if piece == C else ((0, PIECE),):
+                interleave(nc.scalar.copy, piece, 1, c0, c1 - c0)
             quantise(piece, 1, PIECE)
             at = (piece - C) * PIECE
             product(FIRST, piece, PIECE, None, BY_K[2:], first_late[:, at : at + PIECE], False, piece == D)

@@ -214,29 +214,32 @@ def tile_list_embg_res_noneP_kernel(
         for n, t in enumerate((THIRD, SECOND)):
             product(t, B, PIECE, None, into=both[:, 0, n * PIECE : (n + 1) * PIECE])
         product(LAST, A, HALF, None, into=both[:, 1, :])
-        product(FIRST, C, HALF, "bank4", BY_K[:2], closes=False)
-        first_late = bank[FIRST, C]
+        first_late = {}
+        for piece in (C, D):
+            product(FIRST, piece, PIECE, f"bank{piece + 2}", BY_K[:2], closes=False)
+            first_late[piece] = bank[FIRST, piece]
         for piece in (C, D):
             for c0, c1 in ((0, PIECE // 2), (PIECE // 2, PIECE)) if piece == C else ((0, PIECE),):
                 interleave(nc.scalar.copy, piece, 1, c0, c1 - c0)
             quantise(piece, 1, PIECE)
-            at = (piece - C) * PIECE
-            product(FIRST, piece, PIECE, None, BY_K[2:], first_late[:, at : at + PIECE], False, piece == D)
-        bank[FIRST, C] = first_late
-        held = sb("dx_held", [P, 4, PIECE], F32, f"raw{D}1")
-        nc.scalar.copy(out=held[:, 0:2, :].rearrange("p n c -> p (n c)"), in_=both[:, 0, :])
-        dx_last = sb("dx_last", [P, J], F32, f"g{C}1")
-        empty_bank(nc.scalar.copy, LAST, A, dx_last[:, 0:HALF])
-        dx[THIRD, B] = held[:, 0, :]
+            product(FIRST, piece, PIECE, None, BY_K[2:], first_late[piece], opens=False)
+        dx[THIRD, B] = sb("dx_tb", [P, PIECE], F32, f"raw{D}1")[:]
+        nc.scalar.copy(out=dx[THIRD, B], in_=both[:, 0, 0:PIECE])
         scatter(THIRD, B, PIECE)
+        held = sb("dx_held", [P, HALF + J - PIECE], F32, f"g{C}1")
+        empty_bank(nc.scalar.copy, FIRST, C, held[:, 0:PIECE])
+        dx[SECOND, B] = held[:, HALF:]
+        nc.scalar.copy(out=dx[SECOND, B][:, 0:PIECE], in_=both[:, 0, PIECE:HALF])
+        empty_bank(nc.scalar.copy, FIRST, D, held[:, PIECE:HALF])
+        dx[FIRST, C] = held[:, 0:HALF]
+        dx_last = sb("dx_last", [P, J], F32, f"raw{D}1")
+        empty_bank(nc.scalar.copy, LAST, A, dx_last[:, 0:HALF])
 
-        empty_bank(nc.scalar.copy, FIRST, C, sb("dx_first_late", [P, HALF], F32)[:])
-        product(THIRD, C, HALF, "bank0")
+        product(THIRD, C, HALF, f"bank{D + 2}")
         empty_bank(nc.scalar.copy, THIRD, C, sb("dx_third_late", [P, HALF], F32)[:])
-        product(SECOND, C, HALF, "bank4")
-        empty_bank(nc.scalar.copy, SECOND, C, held[:, 2:4, :].rearrange("p n c -> p (n c)"))
-        dx[SECOND, B] = held[:, 1:4, :].rearrange("p n c -> p (n c)")
-        product(LAST, C, HALF, "bank0")
+        product(SECOND, C, HALF, "bank0")
+        empty_bank(nc.scalar.copy, SECOND, C, dx[SECOND, B][:, PIECE:])
+        product(LAST, C, HALF, f"bank{D + 2}")
         empty_bank(nc.scalar.copy, LAST, C, dx_last[:, HALF:J])
 
         out_rows = out_0.rearrange("(p t) c -> p t c", t=PACK)

@@ -80,8 +80,8 @@ def tile_list_embg_res_noneP_kernel(
         for a in range(PASSES):
             load_dy(B, a)
         nc.sync.dma_start(out=wgo_sb[:, PIECE:HALF], in_=wgo[:, PIECE:HALF])
-        for a in range(PASSES):
-            for piece in (C, D):
+        for piece in (C, D):
+            for a in range(PASSES):
                 load_dy(piece, a)
         nc.sync.dma_start(out=wgo_sb[:, HALF:J], in_=wgo[:, HALF:J])
 
@@ -134,7 +134,7 @@ def tile_list_embg_res_noneP_kernel(
 
         bank = {}
 
-        def product(t, piece, width, tag, order=BY_K, into=None, opens=True, closes=True):
+        def product(t, piece, width, tag, order=BY_K, into=None):
             h, c0 = divmod(piece * PIECE, HALF)
             cols = slice(c0, c0 + width)
             bank[t, piece] = into if tag is None else psum.tile([P, width], F32, name=f"bank{t}{piece}", tag=tag)
@@ -150,8 +150,8 @@ def tile_list_embg_res_noneP_kernel(
                     lhsT_scale=bytes_of_scale,
                     rhs=codes[h, a][:, cols].bitcast(E5M2X4),
                     rhs_scale=scales[h, a][:, cols],
-                    start=(opens and step == 0),
-                    stop=(closes and step == len(order) - 1),
+                    start=(step == 0),
+                    stop=(step == len(order) - 1),
                 )
 
         dx = {}
@@ -194,52 +194,54 @@ def tile_list_embg_res_noneP_kernel(
         nc.gpsimd.memset(window[THIRD][:], 0.0)
 
         product(FIRST, A, PIECE, "bank0", ((4, 0), (4, 1), (8, 0), (8, 1)))
+        behind_w8 = ((4, 0), (8, 0), (8, 1), (4, 1))
         for n, t in enumerate((SECOND, THIRD)):
-            product(t, A, PIECE, f"bank{1 + n}", ((4, 0), (8, 0), (8, 1), (4, 1)))
+            product(t, A, PIECE, f"bank{1 + n}", behind_w8)
+        last_ab = psum.tile([P, 2, PIECE], F32, name="last_ab", tag="bank3")
+        product(LAST, A, PIECE, None, behind_w8, last_ab[:, 0, :])
         empty_bank(nc.vector.tensor_copy, FIRST, A, sb("dx_fa", [P, PIECE], F32)[:])
         scatter(FIRST, A, PIECE)
-        for a, (t, tag) in enumerate(((SECOND, None), (THIRD, f"raw{B}0"))):
+        for a in range(PASSES):
             interleave(nc.scalar.copy, B, a, 0, PIECE)
             quantise(B, a, PIECE)
-            empty_bank(nc.scalar.copy, t, A, sb(f"dx_early{t}", [P, PIECE], F32, tag)[:])
+        early = sb("dx_early", [P, 2, PIECE], F32, f"raw{B}1")
+        for n, t in enumerate((SECOND, THIRD)):
+            empty_bank(nc.scalar.copy, t, A, early[:, n, :])
             scatter(t, A, PIECE)
-        product(FIRST, B, PIECE, "bank3")
-        interleave(nc.scalar.copy, C, 0, 0, PIECE)
-        interleave(nc.scalar.copy, D, 0, 0, PIECE)
-        quantise(C, 0, HALF)
-        empty_bank(nc.scalar.copy, FIRST, B, sb("dx_fb", [P, PIECE], F32, f"raw{D}0")[:])
+        product(FIRST, B, PIECE, "bank0")
+        others_b = psum.tile([P, 2, PIECE], F32, name="others_b", tag="bank4")
+        for n, t in enumerate((THIRD, SECOND)):
+            product(t, B, PIECE, None, into=others_b[:, n, :])
+        product(LAST, B, PIECE, None, into=last_ab[:, 1, :])
+        for a in range(PASSES):
+            interleave(nc.scalar.copy, C, a, 0, PIECE)
+            quantise(C, a, PIECE)
+        empty_bank(nc.scalar.copy, FIRST, B, sb("dx_fb", [P, PIECE], F32, f"raw{C}0")[:])
         scatter(FIRST, B, PIECE)
 
-        both = psum.tile([P, 2, HALF], F32, name="both", tag="bank0")
-        for n, t in enumerate((THIRD, SECOND)):
-            product(t, B, PIECE, None, into=both[:, 0, n * PIECE : (n + 1) * PIECE])
-        product(LAST, A, HALF, None, into=both[:, 1, :])
-        first_late = {}
-        for piece in (C, D):
-            product(FIRST, piece, PIECE, f"bank{piece + 2}", BY_K[:2], closes=False)
-            first_late[piece] = bank[FIRST, piece]
-        for piece in (C, D):
-            for c0, c1 in ((0, PIECE // 2), (PIECE // 2, PIECE)) if piece == C else ((0, PIECE),):
-                interleave(nc.scalar.copy, piece, 1, c0, c1 - c0)
-            quantise(piece, 1, PIECE)
-            product(FIRST, piece, PIECE, None, BY_K[2:], first_late[piece], opens=False)
-        dx[THIRD, B] = sb("dx_tb", [P, PIECE], F32, f"raw{D}1")[:]
-        nc.scalar.copy(out=dx[THIRD, B], in_=both[:, 0, 0:PIECE])
-        scatter(THIRD, B, PIECE)
-        held = sb("dx_held", [P, HALF + J - PIECE], F32, f"g{C}1")
+        product(FIRST, C, PIECE, "bank1")
+        third_cd = psum.tile([P, 2, PIECE], F32, name="third_cd", tag="bank2")
+        product(THIRD, C, PIECE, None, into=third_cd[:, 0, :])
+        for a in range(PASSES):
+            interleave(nc.scalar.copy, D, a, 0, PIECE)
+            quantise(D, a, PIECE)
+        product(FIRST, D, PIECE, "bank5")
+        product(THIRD, D, PIECE, None, into=third_cd[:, 1, :])
+        held = sb("dx_held", [P, 2 * PIECE + J - PIECE], F32, f"raw{D}1")
         empty_bank(nc.scalar.copy, FIRST, C, held[:, 0:PIECE])
+        scatter(FIRST, C, PIECE)
+        dx[THIRD, B] = held[:, PIECE:HALF]
         dx[SECOND, B] = held[:, HALF:]
-        nc.scalar.copy(out=dx[SECOND, B][:, 0:PIECE], in_=both[:, 0, PIECE:HALF])
-        empty_bank(nc.scalar.copy, FIRST, D, held[:, PIECE:HALF])
-        dx[FIRST, C] = held[:, 0:HALF]
-        dx_last = sb("dx_last", [P, J], F32, f"raw{D}1")
-        empty_bank(nc.scalar.copy, LAST, A, dx_last[:, 0:HALF])
-
-        product(THIRD, C, HALF, f"bank{D + 2}")
-        empty_bank(nc.scalar.copy, THIRD, C, sb("dx_third_late", [P, HALF], F32)[:])
-        product(SECOND, C, HALF, "bank0")
+        nc.scalar.copy(out=held[:, PIECE : PIECE + HALF], in_=others_b[:].rearrange("p n c -> p (n c)"))
+        scatter(THIRD, B, PIECE)
+        dx_last = sb("dx_last", [P, J], F32, f"g{C}1")
+        nc.scalar.copy(out=dx_last[:, 0:HALF], in_=last_ab[:].rearrange("p n c -> p (n c)"))
+        empty_bank(nc.scalar.copy, FIRST, D, sb("dx_fd", [P, PIECE], F32)[:])
+        dx[THIRD, C] = sb("dx_third_late", [P, HALF], F32)[:]
+        nc.scalar.copy(out=dx[THIRD, C], in_=third_cd[:].rearrange("p n c -> p (n c)"))
+        product(SECOND, C, HALF, "bank5")
         empty_bank(nc.scalar.copy, SECOND, C, dx[SECOND, B][:, PIECE:])
-        product(LAST, C, HALF, f"bank{D + 2}")
+        product(LAST, C, HALF, "bank2")
         empty_bank(nc.scalar.copy, LAST, C, dx_last[:, HALF:J])
 
         out_rows = out_0.rearrange("(p t) c -> p t c", t=PACK)
@@ -271,7 +273,7 @@ def tile_list_embg_res_noneP_kernel(
                 in_=words.rearrange("p u (c l) -> p c u l", l=LINE),
             )
 
-        for t, piece in ((FIRST, C), (THIRD, C), (SECOND, B)):
+        for t, piece in ((FIRST, D), (THIRD, C), (SECOND, B)):
             scatter(t, piece, J - piece * PIECE)
             nc.sync.dma_start(out=out_rows[:, t, :], in_=window[t][:])
             for c0, c1 in runs(0, VECTOR_TAIL, HALF):

@@ -197,8 +197,6 @@ def tile_list_embg_res_noneP_kernel(
         behind_w8 = ((4, 0), (8, 0), (8, 1), (4, 1))
         for n, t in enumerate((SECOND, THIRD)):
             product(t, A, PIECE, f"bank{1 + n}", behind_w8)
-        last_ab = psum.tile([P, 2, PIECE], F32, name="last_ab", tag="bank3")
-        product(LAST, A, PIECE, None, behind_w8, last_ab[:, 0, :])
         empty_bank(nc.vector.tensor_copy, FIRST, A, sb("dx_fa", [P, PIECE], F32)[:])
         scatter(FIRST, A, PIECE)
         for a in range(PASSES):
@@ -212,14 +210,16 @@ def tile_list_embg_res_noneP_kernel(
         others_b = psum.tile([P, 2, PIECE], F32, name="others_b", tag="bank4")
         for n, t in enumerate((THIRD, SECOND)):
             product(t, B, PIECE, None, into=others_b[:, n, :])
-        product(LAST, B, PIECE, None, into=last_ab[:, 1, :])
+        last_ab = psum.tile([P, 2, PIECE], F32, name="last_ab", tag="bank1")
+        for piece in (A, B):
+            product(LAST, piece, PIECE, None, into=last_ab[:, piece, :])
         for a in range(PASSES):
             interleave(nc.scalar.copy, C, a, 0, PIECE)
             quantise(C, a, PIECE)
         empty_bank(nc.scalar.copy, FIRST, B, sb("dx_fb", [P, PIECE], F32, f"raw{C}0")[:])
         scatter(FIRST, B, PIECE)
 
-        product(FIRST, C, PIECE, "bank1")
+        product(FIRST, C, PIECE, "bank3")
         third_cd = psum.tile([P, 2, PIECE], F32, name="third_cd", tag="bank2")
         product(THIRD, C, PIECE, None, into=third_cd[:, 0, :])
         for a in range(PASSES):
@@ -245,7 +245,7 @@ def tile_list_embg_res_noneP_kernel(
         empty_bank(nc.scalar.copy, LAST, C, dx_last[:, HALF:J])
 
         out_rows = out_0.rearrange("(p t) c -> p t c", t=PACK)
-        pairs = [sb(f"pairs{c}", [P, 2, HALF, 2], BF16, ("codes1", "scales1")[c // 2] + str(c % 2)) for c in range(T // HALF)]
+        pairs = [sb(f"pairs{c}", [P, 2, T // 2, 2], BF16, tag) for c, tag in enumerate(("codes11", "scales11"))]
 
         grouped = [sb(f"grouped{c}", [P, CHUNK, PACK], BF16) for c in range(CHUNKS)]
 
@@ -254,18 +254,18 @@ def tile_list_embg_res_noneP_kernel(
             return list(zip(edges[:-1], edges[1:]))
 
         def round_plane(copy, t, c0, c1):
-            c, at = divmod(c0, HALF)
+            c, at = divmod(c0, T // 2)
             copy(out=pairs[c][:, t // 2, at : at + c1 - c0, t % 2], in_=window[t][:, c0:c1])
 
         def round_into_both_halves(t, c0, c1):
-            c, at = divmod(c0, HALF)
+            c, at = divmod(c0, T // 2)
             nc.scalar.copy(
                 out=pairs[c][:, t // 2, at : at + c1 - c0, :],
                 in_=window[t][:, c0:c1].unsqueeze(2).to_broadcast([P, c1 - c0, 2]),
             )
 
         def weave(copy, c0, c1):
-            c, at = divmod(c0, HALF)
+            c, at = divmod(c0, T // 2)
             k, to = divmod(c0, CHUNK)
             words = pairs[c][:].rearrange("p u c e -> p u (c e)").bitcast(F32)[:, :, at : at + c1 - c0]
             copy(

@@ -247,7 +247,12 @@ def tile_list_embg_res_noneP_kernel(
         out_rows = out_0.rearrange("(p t) c -> p t c", t=PACK)
         pairs = [sb(f"pairs{c}", [P, 2, T // 2, 2], BF16, tag) for c, tag in enumerate(("codes11", "scales11"))]
 
-        grouped = [sb(f"grouped{c}", [P, CHUNK, PACK], BF16) for c in range(CHUNKS)]
+        starts = [0, HALF] + list(range(2 * HALF, T, CHUNK))
+        grouped = {c0: sb(f"grouped{c0}", [P, c1 - c0, PACK], BF16) for c0, c1 in zip(starts, starts[1:] + [T])}
+
+        def grouped_columns(c0, c1):
+            first = max(start for start in starts if start <= c0)
+            return grouped[first][:, c0 - first : c1 - first, :]
 
         def runs(c0, c1, size):
             edges = [c0] + list(range((c0 // size + 1) * size, c1, size)) + [c1]
@@ -266,10 +271,9 @@ def tile_list_embg_res_noneP_kernel(
 
         def weave(copy, c0, c1):
             c, at = divmod(c0, T // 2)
-            k, to = divmod(c0, CHUNK)
             words = pairs[c][:].rearrange("p u c e -> p u (c e)").bitcast(F32)[:, :, at : at + c1 - c0]
             copy(
-                out=grouped[k][:].bitcast(F32)[:, to : to + c1 - c0, :].rearrange("p (c l) u -> p c u l", l=LINE),
+                out=grouped_columns(c0, c1).bitcast(F32).rearrange("p (c l) u -> p c u l", l=LINE),
                 in_=words.rearrange("p u (c l) -> p c u l", l=LINE),
             )
 
@@ -297,16 +301,15 @@ def tile_list_embg_res_noneP_kernel(
             nc.vector.quantize_mx(
                 out=out_codes[c][:, at : at + CHUNK].bitcast(E4M3X4),
                 scales=out_scales[4 * c : P, at : at + CHUNK],
-                in_=grouped[k][:].rearrange("p c i -> p (c i)"),
+                in_=grouped_columns(k * CHUNK, (k + 1) * CHUNK).rearrange("p c i -> p (c i)"),
             )
 
         for c0, c1 in runs(0, VECTOR_TAIL, HALF):
             round_plane(nc.vector.tensor_copy, LAST, c0, c1)
-        for c0, c1 in runs(0, VECTOR_TAIL, CHUNK):
+        for c0, c1 in runs(0, VECTOR_TAIL, HALF):
             weave(nc.vector.tensor_copy, c0, c1)
         for c0, c1 in runs(VECTOR_TAIL, T, CHUNK):
-            k, to = divmod(c0, CHUNK)
-            nc.scalar.copy(out=grouped[k][:, to : to + c1 - c0, LAST], in_=window[LAST][:, c0:c1])
+            nc.scalar.copy(out=grouped_columns(c0, c1)[:, :, LAST], in_=window[LAST][:, c0:c1])
         for k in range(CHUNKS):
             finish(k)
             if k % 2 == 1:

@@ -247,7 +247,7 @@ def tile_list_embg_res_noneP_kernel(
         out_rows = out_0.rearrange("(p t) c -> p t c", t=PACK)
         pairs = [sb(f"pairs{c}", [P, 2, T // 2, 2], BF16, tag) for c, tag in enumerate(("codes11", "scales11"))]
 
-        starts = [0, HALF] + list(range(2 * HALF, T, CHUNK))
+        starts = [0, HALF, T - HALF, T - CHUNK]
         grouped = {c0: sb(f"grouped{c0}", [P, c1 - c0, PACK], BF16) for c0, c1 in zip(starts, starts[1:] + [T])}
 
         def grouped_columns(c0, c1):
@@ -287,7 +287,7 @@ def tile_list_embg_res_noneP_kernel(
                     round_into_both_halves(t, c0, c1)
                 else:
                     round_plane(nc.scalar.copy, t, c0, c1)
-        for c0, c1 in runs(VECTOR_TAIL, T, CHUNK):
+        for c0, c1 in runs(VECTOR_TAIL, T - HALF, HALF) + runs(T - HALF, T, CHUNK):
             weave(nc.scalar.copy, c0, c1)
         nc.vector.tensor_tensor(window[LAST][:].indirect(offsets[:]), dx_last[:], wgo_sb[:], MULT)
         nc.sync.dma_start(out=out_rows[:, LAST, :], in_=window[LAST][:])
@@ -308,7 +308,7 @@ def tile_list_embg_res_noneP_kernel(
             round_plane(nc.vector.tensor_copy, LAST, c0, c1)
         for c0, c1 in runs(0, VECTOR_TAIL, HALF):
             weave(nc.vector.tensor_copy, c0, c1)
-        for c0, c1 in runs(VECTOR_TAIL, T, CHUNK):
+        for c0, c1 in [(VECTOR_TAIL, T - HALF)] + runs(T - HALF, T, CHUNK):
             nc.scalar.copy(out=grouped_columns(c0, c1)[:, :, LAST], in_=window[LAST][:, c0:c1])
         for k in range(CHUNKS):
             finish(k)

from contextlib import ExitStack

import concourse.mybir as mybir

K, N, T, J = 1024, 512, 2048, 1024
FLOPS = 2 * 2 * K * N * J

F32 = mybir.dt.float32
BF16 = mybir.dt.bfloat16
I32 = mybir.dt.int32
U32 = mybir.dt.uint32
U16 = mybir.dt.uint16
U8 = mybir.dt.uint8
E4M3X4 = mybir.dt.float8_e4m3fn_x4
E5M2X4 = mybir.dt.float8_e5m2_x4
E2M1X4 = mybir.dt.float4_e2m1fn_x4
MULT = mybir.AluOpType.mult

P = 128
PACK = 4
K_PASS = P * PACK
PASSES = K // K_PASS
HALF = 512
PIECE = 256
CHUNK = 256
CHUNKS = T // CHUNK
LINE = 4
VECTOR_COLS = 128
ODD = T // 2 - 1
VECTOR_TAIL = 896
FIRST, SECOND, THIRD, LAST = 0, 2, 3, 1
A, B, C, D = range(4)
BY_K = ((4, 0), (8, 0), (4, 1), (8, 1))


def tile_list_embg_res_noneP_kernel(
    tc, dy, w4_words, w4_scales, w8_words, w8_scales, wgo, offs, out_0, out_1, out_2
):
    nc = tc.nc
    with ExitStack() as ctx:
        listp = ctx.enter_context(tc.tile_pool(name="listp", bufs=1))
        keep = ctx.enter_context(tc.tile_pool(name="keep", bufs=1))
        psum = ctx.enter_context(tc.psum_pool(name="psum", bufs=1))

        def sb(name, shape, dtype, tag=None):
            return keep.tile(shape, dtype, name=name, tag=tag or name, align_bytes=64)

        offsets = listp.tile([P, J // 16], U16, name="offsets")

        s4_raw = sb("s4_raw", [P, PASSES, N], U8)
        s8_raw = sb("s8_raw", [P, PASSES, N], U8)
        nc.gpsimd.memset(s4_raw[:].rearrange("p a n -> p (a n)").bitcast(I32), 0)
        nc.gpsimd.memset(s8_raw[:].rearrange("p a n -> p (a n)").bitcast(I32), 0)

        raw = {}

        def load_dy(piece, a):
            raw[piece, a] = sb(f"raw{piece}{a}", [P, PACK, PIECE], F32)
            rows = dy[a * K_PASS : (a + 1) * K_PASS, piece * PIECE : (piece + 1) * PIECE]
            nc.sync.dma_start(out=raw[piece, a][:], in_=rows.rearrange("(p i) j -> p i j", i=PACK))

        def load_scales(dst, src):
            for q in range(4):
                nc.sync.dma_start(
                    out=dst[32 * q : 32 * q + 4, :, :].bitcast(I32),
                    in_=src[:, 4 * q : 4 * q + 4, :].rearrange("a r n -> r a n").bitcast(I32),
                )

        load_dy(A, 0)
        nc.sync.dma_start(offsets[:], offs)
        w4_raw = sb("w4_raw", [P, PASSES, 2 * N], U8)
        nc.sync.dma_start(out=w4_raw[:].bitcast(I32), in_=w4_words.rearrange("a p b -> p a b").bitcast(I32))
        load_scales(s4_raw, w4_scales)
        load_dy(A, 1)
        w8_raw = sb("w8_raw", [P, PASSES, N], I32)
        nc.sync.dma_start(out=w8_raw[:], in_=w8_words.rearrange("a p n i -> p a (n i)").bitcast(I32))
        load_scales(s8_raw, w8_scales)
        wgo_sb = sb("wgo_sb", [P, J], F32)
        nc.sync.dma_start(out=wgo_sb[:, 0:PIECE], in_=wgo[:, 0:PIECE])
        for a in range(PASSES):
            load_dy(B, a)
        nc.sync.dma_start(out=wgo_sb[:, PIECE:HALF], in_=wgo[:, PIECE:HALF])
        for piece in (C, D):
            for a in range(PASSES):
                load_dy(piece, a)
        nc.sync.dma_start(out=wgo_sb[:, HALF:J], in_=wgo[:, HALF:J])

        window = {}
        for t in (FIRST, SECOND):
            window[t] = sb(f"window{t}", [P, T], F32)
        nc.vector.memset(window[FIRST][:, 0:ODD], 0.0)
        nc.vector.memset(window[FIRST][:, ODD:T], 0.0)
        nc.gpsimd.memset(window[SECOND][:], 0.0)
        window[LAST] = window[FIRST]

        grouped_dy = {}

        def interleave(copy, piece, a, c0, width):
            first = min(piece, C)
            if (first, a) not in grouped_dy:
                grouped_dy[first, a] = sb(f"g{first}{a}", [P, HALF if first == C else PIECE, PACK], BF16)
            at = (piece - first) * PIECE + c0
            copy(
                out=grouped_dy[first, a][:, at : at + width, :].rearrange("p (c l) i -> p c i l", l=LINE),
                in_=raw[piece, a][:, :, c0 : c0 + width].rearrange("p i (c l) -> p c i l", l=LINE),
            )

        codes = {}
        scales = {}
        for h in range(2):
            for a in range(PASSES):
                codes[h, a] = sb(f"codes{h}{a}", [P, HALF], U32)
                scales[h, a] = sb(f"scales{h}{a}", [P, HALF], U8)

        def quantise(piece, a, width):
            h, c0 = divmod(piece * PIECE, HALF)
            first = min(piece, C)
            at = (piece - first) * PIECE
            nc.vector.quantize_mx(
                out=codes[h, a][:, c0 : c0 + width].bitcast(E5M2X4),
                scales=scales[h, a][:, c0 : c0 + width],
                in_=grouped_dy[first, a][:, at : at + width, :].rearrange("p c i -> p (c i)"),
            )

        w4_t = sb("w4_t", [P, PACK, PASSES, 2 * P], U8)
        s4_t = sb("s4_t", [P, PACK, PASSES, P], U8)
        w8_first = sb("w8_first", [P, 1, PASSES, P], U32)
        s8_first = sb("s8_first", [P, 1, PASSES, P], U8)
        w8_rest = sb("w8_rest", [P, PACK - 1, PASSES, P], U32)
        s8_rest = sb("s8_rest", [P, PACK - 1, PASSES, P], U8)

        def w8_slice(first, rest, t, a):
            return first[:, 0, a, :] if t == FIRST else rest[:, t - 1, a, :]

        bank = {}

        def product(t, piece, width, tag, order=BY_K, into=None):
            h, c0 = divmod(piece * PIECE, HALF)
            cols = slice(c0, c0 + width)
            bank[t, piece] = into if tag is None else psum.tile([P, width], F32, name=f"bank{t}{piece}", tag=tag)
            for step, (bits, a) in enumerate(order):
                if bits == 4:
                    words, bytes_of_scale = w4_t[:, t, a, :].bitcast(E2M1X4), s4_t[:, t, a, :]
                else:
                    words = w8_slice(w8_first, w8_rest, t, a).bitcast(E4M3X4)
                    bytes_of_scale = w8_slice(s8_first, s8_rest, t, a)
                nc.tensor.matmul_mx(
                    out=bank[t, piece][:],
                    lhsT=words,
                    lhsT_scale=bytes_of_scale,
                    rhs=codes[h, a][:, cols].bitcast(E5M2X4),
                    rhs_scale=scales[h, a][:, cols],
                    start=(step == 0),
                    stop=(step == len(order) - 1),
                )

        dx = {}

        def empty_bank(copy, t, piece, dst):
            dx[t, piece] = dst
            copy(out=dst, in_=bank[t, piece][:])

        def scatter(t, piece, width):
            j0 = piece * PIECE
            nc.vector.tensor_tensor(
                window[t][:].indirect(offsets[:, j0 // 16 : (j0 + width) // 16]),
                dx[t, piece],
                wgo_sb[:, j0 : j0 + width],
                MULT,
            )

        nc.scalar.copy(
            out=w4_t[:].bitcast(U16).rearrange("p t a m -> p a m t"),
            in_=w4_raw[:].bitcast(U16).rearrange("p a (m t) -> p a m t", t=PACK),
        )
        interleave(nc.vector.tensor_copy, A, 0, 0, PIECE)
        quantise(A, 0, PIECE)
        nc.vector.tensor_copy(out=s4_t[:], in_=s4_raw[:].rearrange("p a (m t) -> p t a m", t=PACK))
        interleave(nc.vector.tensor_copy, A, 1, 0, VECTOR_COLS)
        interleave(nc.scalar.copy, A, 1, VECTOR_COLS, PIECE - VECTOR_COLS)
        quantise(A, 1, PIECE)
        w8_by_slice = w8_raw[:].bitcast(U32).rearrange("p a (m t) -> p a m t", t=PACK)
        s8_by_slice = s8_raw[:].rearrange("p a (m t) -> p t a m", t=PACK)
        nc.vector.tensor_copy(
            out=w8_first[:].bitcast(I32), in_=w8_raw[:].rearrange("p a (m t) -> p t a m", t=PACK)[:, 0:1]
        )
        nc.scalar.copy(out=w8_rest[:].rearrange("p t a m -> p a m t"), in_=w8_by_slice[:, :, :, 1:PACK])
        nc.vector.tensor_copy(out=s8_first[:], in_=s8_by_slice[:, 0:1])
        nc.vector.tensor_copy(
            out=s8_rest[:].rearrange("p t a m -> p a t m"),
            in_=s8_raw[:].rearrange("p a (m t) -> p a t m", t=PACK)[:, :, 1:PACK],
        )
        window[THIRD] = sb("third_window", [P, T], F32, "s8_raw")
        nc.gpsimd.memset(window[THIRD][:], 0.0)

        product(FIRST, A, PIECE, "bank0", ((4, 0), (4, 1), (8, 0), (8, 1)))
        behind_w8 = ((4, 0), (8, 0), (8, 1), (4, 1))
        for n, t in enumerate((SECOND, THIRD)):
            product(t, A, PIECE, f"bank{1 + n}", behind_w8)
        empty_bank(nc.vector.tensor_copy, FIRST, A, sb("dx_fa", [P, PIECE], F32)[:])
        scatter(FIRST, A, PIECE)
        for a in range(PASSES):
            interleave(nc.scalar.copy, B, a, 0, PIECE)
            quantise(B, a, PIECE)
        early = sb("dx_early", [P, 2, PIECE], F32, f"raw{B}1")
        for n, t in enumerate((SECOND, THIRD)):
            empty_bank(nc.scalar.copy, t, A, early[:, n, :])
            scatter(t, A, PIECE)
        product(FIRST, B, PIECE, "bank0")
        others_b = psum.tile([P, 2, PIECE], F32, name="others_b", tag="bank4")
        for n, t in enumerate((THIRD, SECOND)):
            product(t, B, PIECE, None, into=others_b[:, n, :])
        last_ab = psum.tile([P, 2, PIECE], F32, name="last_ab", tag="bank1")
        for piece in (A, B):
            product(LAST, piece, PIECE, None, into=last_ab[:, piece, :])
        for a in range(PASSES):
            interleave(nc.scalar.copy, C, a, 0, PIECE)
            quantise(C, a, PIECE)
        empty_bank(nc.scalar.copy, FIRST, B, sb("dx_fb", [P, PIECE], F32, f"raw{C}0")[:])
        scatter(FIRST, B, PIECE)

        product(FIRST, C, PIECE, "bank3")
        third_cd = psum.tile([P, 2, PIECE], F32, name="third_cd", tag="bank2")
        product(THIRD, C, PIECE, None, into=third_cd[:, 0, :])
        for a in range(PASSES):
            interleave(nc.scalar.copy, D, a, 0, PIECE)
            quantise(D, a, PIECE)
        product(FIRST, D, PIECE, "bank5")
        product(THIRD, D, PIECE, None, into=third_cd[:, 1, :])
        held = sb("dx_held", [P, 2 * PIECE + J - PIECE], F32, f"raw{D}1")
        empty_bank(nc.scalar.copy, FIRST, C, held[:, 0:PIECE])
        scatter(FIRST, C, PIECE)
        dx[THIRD, B] = held[:, PIECE:HALF]
        dx[SECOND, B] = held[:, HALF:]
        nc.scalar.copy(out=held[:, PIECE : PIECE + HALF], in_=others_b[:].rearrange("p n c -> p (n c)"))
        scatter(THIRD, B, PIECE)
        dx_last = sb("dx_last", [P, J], F32, f"g{C}1")
        nc.scalar.copy(out=dx_last[:, 0:HALF], in_=last_ab[:].rearrange("p n c -> p (n c)"))
        empty_bank(nc.scalar.copy, FIRST, D, sb("dx_fd", [P, PIECE], F32)[:])
        dx[THIRD, C] = sb("dx_third_late", [P, HALF], F32)[:]
        nc.scalar.copy(out=dx[THIRD, C], in_=third_cd[:].rearrange("p n c -> p (n c)"))
        product(SECOND, C, HALF, "bank5")
        empty_bank(nc.scalar.copy, SECOND, C, dx[SECOND, B][:, PIECE:])
        product(LAST, C, HALF, "bank2")
        empty_bank(nc.scalar.copy, LAST, C, dx_last[:, HALF:J])

        out_rows = out_0.rearrange("(p t) c -> p t c", t=PACK)
        pairs = [sb(f"pairs{c}", [P, 2, T // 2, 2], BF16, tag) for c, tag in enumerate(("codes11", "scales11"))]

        starts = [0, HALF, T - HALF, T - CHUNK]
        grouped = {c0: sb(f"grouped{c0}", [P, c1 - c0, PACK], BF16) for c0, c1 in zip(starts, starts[1:] + [T])}

        def grouped_columns(c0, c1):
            first = max(start for start in starts if start <= c0)
            return grouped[first][:, c0 - first : c1 - first, :]

        def runs(c0, c1, size):
            edges = [c0] + list(range((c0 // size + 1) * size, c1, size)) + [c1]
            return list(zip(edges[:-1], edges[1:]))

        def round_plane(copy, t, c0, c1):
            c, at = divmod(c0, T // 2)
            copy(out=pairs[c][:, t // 2, at : at + c1 - c0, t % 2], in_=window[t][:, c0:c1])

        def round_into_both_halves(t, c0, c1):
            c, at = divmod(c0, T // 2)
            nc.scalar.copy(
                out=pairs[c][:, t // 2, at : at + c1 - c0, :],
                in_=window[t][:, c0:c1].unsqueeze(2).to_broadcast([P, c1 - c0, 2]),
            )

        def weave(copy, c0, c1):
            c, at = divmod(c0, T // 2)
            words = pairs[c][:].rearrange("p u c e -> p u (c e)").bitcast(F32)[:, :, at : at + c1 - c0]
            copy(
                out=grouped_columns(c0, c1).bitcast(F32).rearrange("p (c l) u -> p c u l", l=LINE),
                in_=words.rearrange("p u (c l) -> p c u l", l=LINE),
            )

        for t, piece in ((FIRST, D), (THIRD, C), (SECOND, B)):
            scatter(t, piece, J - piece * PIECE)
            nc.sync.dma_start(out=out_rows[:, t, :], in_=window[t][:])
            for c0, c1 in runs(0, VECTOR_TAIL, HALF):
                round_plane(nc.scalar.copy, t, c0, c1)
            for c0, c1 in runs(VECTOR_TAIL, T, HALF):
                if t == FIRST:
                    round_into_both_halves(t, c0, c1)
                else:
                    round_plane(nc.scalar.copy, t, c0, c1)
        for c0, c1 in runs(VECTOR_TAIL, T - HALF, HALF) + runs(T - HALF, T, CHUNK):
            weave(nc.scalar.copy, c0, c1)
        nc.vector.tensor_tensor(window[LAST][:].indirect(offsets[:]), dx_last[:], wgo_sb[:], MULT)
        nc.sync.dma_start(out=out_rows[:, LAST, :], in_=window[LAST][:])

        out_scales = sb("out_scales", [P, HALF], U8)
        out_words = out_1[0].rearrange("p c i -> p (c i)").bitcast(I32)
        out_codes = [sb(f"out_codes{c}", [P, HALF], U32) for c in range(T // HALF)]

        def finish(k):
            c, at = divmod(k * CHUNK, HALF)
            nc.vector.quantize_mx(
                out=out_codes[c][:, at : at + CHUNK].bitcast(E4M3X4),
                scales=out_scales[4 * c : P, at : at + CHUNK],
                in_=grouped_columns(k * CHUNK, (k + 1) * CHUNK).rearrange("p c i -> p (c i)"),
            )

        for c0, c1 in runs(0, VECTOR_TAIL, HALF):
            round_plane(nc.vector.tensor_copy, LAST, c0, c1)
        for c0, c1 in runs(0, VECTOR_TAIL, HALF):
            weave(nc.vector.tensor_copy, c0, c1)
        for c0, c1 in [(VECTOR_TAIL, T - HALF)] + runs(T - HALF, T, CHUNK):
            nc.scalar.copy(out=grouped_columns(c0, c1)[:, :, LAST], in_=window[LAST][:, c0:c1])
        for k in range(CHUNKS):
            finish(k)
            if k % 2 == 1:
                c = k // 2
                nc.sync.dma_start(out=out_words[:, c * HALF : (c + 1) * HALF], in_=out_codes[c][:].bitcast(I32))
        for q in range(4):
            nc.scalar.dma_start(
                out=out_2[0, 4 * q : 4 * q + 4, :].bitcast(I32).rearrange("r (c w) -> c r w", c=T // HALF),
                in_=out_scales[32 * q : 32 * q + 16, :].bitcast(I32),
            )
